import numpy as np, ml_dtypes
CORES = [3,11,19,27,35,43,51,59]
N = 8
BF = ml_dtypes.bfloat16
LA, SUB, W, V, VIS, TRY, R1, R2 = 192, 16, 3072, 4096, 4, 3, 8, 13
A = [6, 4, 4, 3]
def levels(rng, n, lo, hi):
    return np.minimum((np.exp2(lo + (hi - lo) * rng.random((N, 8, 1, n))) * rng.random((N, 8, 16, n))).astype(np.int64), 255)
def slots(rng):
    share = rng.choice(np.array([0.3, 0.6, 0.9, 1.0]), (N, 8, 1, LA))
    return np.where(rng.random((N, 8, 16, LA)) < share, rng.integers(0, W, (N, 8, 16, LA)), -1)
def parts(rng):
    return (levels(rng, W, 6.5, 9.0), levels(rng, V, 5.5, 9.0), slots(rng), levels(rng, LA, 6.5, 9.0), rng.integers(1, 256, (N, 8, 16)), rng.integers(0, 256, (N, 8, 16)))
def pack(x, c, s, z, w, p):
    b = lambda v: np.ascontiguousarray(v.reshape(N, 128, -1)).astype(np.float32).astype(BF)
    i = lambda v: np.ascontiguousarray(v.reshape(N, 128, -1)).astype(np.int32)
    return {"x0": b(x), "cl": b(c), "sl": i(s), "z0": b(z), "wt": i(w), "kp": i(p)}
def setup_inputs(rng):
    return pack(*parts(rng))
def setup_inputs_spread(rng):
    x, c, s, z, w, p = parts(rng)
    x, c, z = levels(rng, W, 0.0, 9.0), levels(rng, V, 0.0, 9.0), levels(rng, LA, 0.0, 9.0)
    w = np.clip(np.exp2(8 * rng.random(w.shape)).astype(np.int64), 1, 255); p = np.clip(np.exp2(8 * rng.random(p.shape)).astype(np.int64) - 1, 0, 255)
    return pack(x, c, s, z, w, p)
def setup_inputs_ends(rng):
    e = lambda n, d: 255 * (rng.random((N, 8, 16, n)) < rng.choice(np.array(d), (N, 8, 1, n))).astype(np.int64)
    x, c, z = e(W, [0.3, 0.6, 0.9]), e(V, [0.0, 0.5, 0.9, 1.0]), e(LA, [0.3, 0.6, 0.9])
    r = rng.random((N, 8, 16, LA))
    s = np.where(r < 0.35, -1, np.where(r < 0.7, W - 1, np.where(r < 0.8, 0, rng.integers(0, W, r.shape))))
    w = np.where(rng.random((N, 8, 16)) < 0.5, 1, 255); w[:, :, 13:15] = 1; w[:, :, 15] = 255; w[:, 6] = 255
    p = 255 * rng.integers(0, 2, (N, 8, 16)); p[:, 7, 0] = 255; p[:, 7, 15] = 255; p[:, 7, 1] = 0
    x[..., W - 1] = 255
    for i in (0, LA - 1):
        z[..., i] = 0; z[:, :, 13:, i] = 255; s[:, :, 0, i] = W - 1
    for i in (1, LA - 2): z[..., i] = 255
    for i in (2, LA - 3): z[..., i] = 0
    return pack(x, c, s, z, w, p)
def setup_inputs_corners(rng):
    x, c, s, z, w, p = parts(rng); x[..., 0] = 255; x[..., W - 1] = 0
    kind = rng.integers(0, 10, (N, 8, 1, LA)); kind[..., :10] = np.arange(10); kind[..., LA - 10:] = np.arange(10)
    k = np.arange(16)[:, None]; o = np.argsort(rng.random((N, 8, 16, LA)), axis=2); any_ = rng.integers(0, W, s.shape)
    low = np.arange(LA) < LA // 2
    s = np.where(kind == 0, -1, s); s = np.where(kind == 1, any_, s)
    s = np.where(kind == 2, np.where(k == np.where(low, 13, 15), 0, W - 1), s)
    s = np.where(kind == 3, np.where(o < TRY, 0, W - 1), s); s = np.where(kind == 4, np.where(o < TRY + 1, 0, W - 1), s)
    s = np.where(kind == 5, np.where(k == 15, any_, -1), s); s = np.where(kind == 6, np.where(k == 15, -1, any_), s)
    s = np.where(kind == 7, SUB * np.arange(LA) + any_ % SUB, s); s = np.where(kind == 8, any_[:, :, :1], s)
    z = np.where(kind == 1, 255, z); z = np.where((kind >= 2) & (kind <= 4), np.minimum(z, 254), z); z = np.where((kind == 2) & low, 254, z)
    for q in range(N):
        g = rng.permutation(8)
        c[q, g[:2]] = 0; c[q, g[2:4]] = 255
        w[q, g[0]] = 1; w[q, g[2]] = 255; w[q, g[4]] = 255; w[q, g[5]] = 1; p[q, g[3]] = 0; p[q, g[5]] = 255; p[q, g[6]] = 0
    return pack(x, c, s, z, w, p)
def setup_inputs_ties(rng):
    x, c, s, z, w, p = parts(rng)
    x, c, z = 85 * (x >> 6), 85 * (c >> 6), 85 * (z >> 6)
    x[..., 1::2] = x[..., ::2]
    same = np.take_along_axis(x, np.maximum(s[:, :, 3:4], 0), 3)
    z = np.where(rng.random((N, 8, 1, LA)) < 0.5, same, z)
    return pack(x, c, s, z, w, p)
def setup_inputs_bits(rng):
    x, c, s, z, w, p = parts(rng); k = np.arange(16)[:, None]
    one = k == rng.integers(0, 16, (N, 8, 1, 1))
    x[..., 0] = 255; x[..., W - 2] = 0; x[..., W - 1:] = np.where(one, 255, 0)
    kind = rng.choice(np.array([0, 0, 1, 2, 3, 3]), (N, 1, 1, LA))
    m = np.where(kind == 0, 8, 1 + 2 * rng.integers(0, 4, kind.shape)); on = np.argsort(rng.random((N, 8, 1, LA)), axis=1) < m
    first = np.where(kind == 1, 0, TRY - 1)
    v = np.where(k < first, W - 1, np.where(k == first, 0, s))
    v = np.where(on, v, np.where(rng.random((N, 8, 1, LA)) < 0.5, -1, W - 2))
    s = np.where(kind < 3, v, s)
    high = 255 - (rng.random((N, 8, 16, LA)) < rng.choice(np.array([0.0, 0.5, 1.0]), (N, 1, 1, LA))).astype(np.int64)
    z = np.where(kind < 3, np.where(one, 254, high), z)
    w[:, 7] = 255
    return pack(x, c, s, z, w, p)
def check_inputs(d):
    bad = []
    for k, lo, hi in (("x0", 0, 255), ("cl", 0, 255), ("sl", -1, W - 1), ("z0", 0, 255), ("wt", 1, 255), ("kp", 0, 255)):
        v = np.asarray(d[k]).astype(np.float32)
        if np.min(v) < lo or np.max(v) > hi or np.any(v != np.floor(v)): bad.append("range of " + k)
    return bad
def hashes(v, w, p, t):
    u = np.add.reduce(w * v, axis=2) & (V - 1)
    return u, ((u * u >> 5)[:, :, None] + p * u[:, :, None] + 97 * t) & (V - 1)
def reference(x0, cl, sl, z0, wt, kp):
    x = x0.astype(np.float32).astype(np.int32).reshape(N, 8, 16, W); c = cl.astype(np.float32).astype(np.int32).reshape(N, 8, 16, V)
    z = z0.astype(np.float32).astype(np.int32).reshape(N, 8, 16, LA); s = sl.astype(np.int32).reshape(N, 8, 16, LA)
    w = wt.astype(np.int32).reshape(N, 8, 16, 1); p = kp.astype(np.int32).reshape(N, 8, 16, 1)
    bit = np.zeros((N, LA), np.int64); k16 = np.arange(16)[:, None]
    for t in range(VIS):
        J = (np.arange(N) + 1 + t % (N - 1)) % N
        filled = s >= 0
        old = np.take_along_axis(x, np.maximum(s, 0).reshape(N, 8, 1, 16 * LA), 3).reshape(N, 8, 16, 16, LA)
        m = np.minimum(z[:, :, :, None], old)
        free = filled & (np.add.reduce(m, axis=2) < np.add.reduce(old, axis=2))
        done = np.zeros((N, 8, LA), bool); best = z; put = np.zeros((N, 8, LA), np.int64)
        for trial in range(TRY):
            has = np.any(free, axis=2) & ~done; k = np.argmax(free, axis=2)
            cand = np.take_along_axis(m, k[:, :, None, None], 3)[:, :, :, 0]
            h = hashes(cand, w[J], p[J], t)[1]
            b = np.take_along_axis(c[J], h.reshape(N, 8, 1, 16 * LA), 3).reshape(N, 8, 16, 16, LA)
            met = np.add.reduce((b <= cand[:, :, :, None]).astype(np.int32), axis=2) >= R1
            neg = has & (np.add.reduce(met.astype(np.int32), axis=2) >= A[t] + bit[J][:, None])
            bit[J] = np.add.reduce(neg.astype(np.int64), axis=1) & 1
            best = np.where(neg[:, :, None], cand, best); put = np.where(neg, k, put); done = done | neg
            free = free & (k16 != k[:, :, None])
        put = np.where(done, put, np.where(np.any(~filled, axis=2), np.argmax(~filled, axis=2), t))
        n = SUB * np.arange(LA) + (hashes(best, w, p, t)[0] & (SUB - 1))
        near = filled & (np.add.reduce((old <= best[:, :, :, None]).astype(np.int32), axis=2) >= R2)
        v = np.maximum(best, np.maximum.reduce(np.where(near[:, :, None], old, 0), axis=3))
        h0 = hashes(v, w, p, t)[1][:, :, :1]
        z = np.abs(v - np.take_along_axis(c, h0, 3))
        np.put_along_axis(x, np.ascontiguousarray(np.broadcast_to(n[:, :, None], (N, 8, 16, LA))), best, 3)
        s = np.where(k16 == put[:, :, None], n[:, :, None], s)
    return {"yx": x.reshape(N, 128, W).astype(np.float32).astype(BF), "yl": s.reshape(N, 128, LA).astype(np.float32), "yz": z.reshape(N, 128, LA).astype(np.float32).astype(BF)}

@@ -1,0 +1,709 @@
+from concourse.mybir import AluOpType as OP, ActivationFunctionType as AF
+
+H = 1
+N, LA, W, V, VIS, SUB = 8, 192, 3072, 4096, 4, 16
+A = [6, 4, 4, 3]
+ZB = 3072
+L, C = LA // H, 12 // H
+W3 = 3 * C
+KB = 384 // L
+NB = 16 // KB
+SO = NB // 2
+SN = NB // 2
+M0 = 10
+MG = 144 // W3
+BH = 6 // H
+GV = (tuple(range(0, NB, 2)), ())
+TOL, LEAD = 0.02, 5.0
+
+SCRATCH = {}
+for _n, _c, _d in (("X", W + 16, "bfloat16"), ("CL", V, "bfloat16"), ("ones", 128, "bfloat16"), ("neg", 2048, "bfloat16"), ("R", 2048, "bfloat16"), ("SLh", 144, "bfloat16"), ("c8L", W3, "bfloat16"),
+                   ("I", 128, "bfloat16"), ("nI", 128, "bfloat16"), ("I128", 128, "bfloat16"), ("I3", 128, "bfloat16"), ("I2", 128, "bfloat16"), ("I1", 128, "bfloat16"),
+                   ("spk", 144, "bfloat16"), ("SLa", 144, "bfloat16"), ("SL", 144, "bfloat16"), ("SLL", 144, "bfloat16"),
+                   ("BOa", 128, "bfloat16"), ("BO", 128, "bfloat16"), ("Tri", 128, "bfloat16"), ("Q16", 128, "bfloat16"), ("GR", 128, "bfloat16"),
+                   ("cmk0", 128, "float32"), ("cmk1", 128, "float32"), ("PM00", 128, "float32"), ("PM01", 128, "float32"), ("PM10", 128, "float32"), ("PM11", 128, "float32"),
+                   ("pc", 1, "int32"), ("p15", 1, "int32"), ("p15f", 1, "float32"), ("kempty", 1, "float32"), ("thrn", 1, "float32"), ("thrc", 1, "float32"), ("cols", 8, "float32"),
+                   ("g16", 12, "int32"), ("p15t", 12, "int32"), ("LI", 12, "int32"), ("e12", 12, "int32"), ("q12", 12, "int32"), ("TW", 12, "uint16"), ("TK", 12, "uint16"), ("recb", 12, "float32"),
+                   ("LI3f", W3, "float32"), ("LI3b", W3, "bfloat16"), ("LIb", C, "bfloat16"), ("c3L", C, "bfloat16"), ("KIL", 16 * C, "float32"),
+                   ("sln", LA, "int32"), ("sad", LA, "float32"), ("sae", LA, "float32"), ("T1", LA, "float32"), ("T2", LA, "float32"), ("T3", LA, "float32"), ("T4", LA, "float32"), ("T5", LA, "float32"), ("T6", LA, "float32"),
+                   ("wti", 1, "int32"), ("kpi", 1, "int32"), ("kpf", 1, "float32"), ("kpd", 16, "bfloat16"), ("WK0", 24, "float32"), ("B0", 12, "int32"), ("pint", 12, "int32")):
+    SCRATCH[_n] = ("sbuf", [128, _c], _d)
+for _q in range(1, 5):
+    SCRATCH["BK%d" % _q] = ("sbuf", [128, V], "bfloat16")
+    SCRATCH["WK%d" % _q] = ("sbuf", [128, 24], "float32")
+for _q in range(5):
+    SCRATCH["SW%d" % _q] = ("sbuf", [128, 144], "bfloat16")
+for _t in range(1, VIS):
+    SCRATCH["bs%d" % _t] = ("sbuf", [128, 12], "int32")
+    SCRATCH["bl%d" % _t] = ("sbuf", [128, 12], "int32")
+for _h in range(H):
+    for _n, _c, _d in (("Oa", 17 * L, "bfloat16"), ("Ob", 17 * L, "bfloat16"), ("Ca", 4 * L, "bfloat16"), ("Cb", 4 * L, "bfloat16"), ("cmp", 16 * L, "bfloat16"),
+                       ("op", L, "bfloat16"), ("le", 3 * L, "bfloat16"), ("off", W3, "uint16"), ("kL", W3, "float32"), ("pen", W3, "float32"),
+                       ("ui", W3, "int32"), ("um", W3, "int32"), ("uf", W3, "float32"), ("sq", W3, "int32"), ("ba", W3, "int32"), ("KU", 16 * W3, "float32"), ("Hs", 16 * W3, "int32"), ("Hm", 16 * W3, "int32"), ("ho", 16 * W3, "uint16"),
+                       ("G", 48 * L, "bfloat16"), ("SG", 24 * L, "bfloat16"), ("ge", 3 * L, "bfloat16"), ("cm", W3, "float32"), ("cd", 2 * C, "float32"), ("nb", 6 * C, "bfloat16"), ("bt", 3 * C, "int32"), ("bo", C, "uint16"), ("M", L, "bfloat16"),
+                       ("nn", L, "bfloat16"), ("acc", 384, "bfloat16"), ("fo", 192, "bfloat16"), ("cc", L, "bfloat16"), ("df", L, "bfloat16"), ("ci", 8 * C, "int32"), ("ch", C, "uint16"),
+                       ("s", 16 * C, "float32"), ("s16", 16 * C, "uint16"), ("eq", 16 * C, "float32"), ("dd", 16 * C, "float32"), ("ed", 16 * C, "float32"),
+                       ("mx", 15 * C, "float32"), ("fe", 4 * C, "float32"), ("pu", 3 * C, "float32"), ("ni", 2 * C, "int32"), ("nf", C, "float32"), ("n16", C, "uint16")):
+        SCRATCH["%s_%d" % (_n, _h)] = ("sbuf", [128, _c], _d)
+for _b in range(8):
+    SCRATCH["pb%d" % _b] = ("psum", [128, 512], "float32")
+OWN = ("X", "CL", "sln", "wti", "kpi", "T1", "WK", "BK", "bs", "bl", "Ca", "Cb", "pb", "B0")
+LOGICAL, PLACE = dict(SCRATCH), {}
+_at = {}
+for _n, (_w, _s, _d) in list(SCRATCH.items()):
+    if _n.split("_")[0].rstrip("0123456789") in OWN or _n in OWN:
+        continue
+    _p = "pool_" + _d
+    _u = 16 if _d in ("float32", "int32") else 32
+    PLACE[_n] = (_p, _at.get(_p, 0))
+    _at[_p] = (_at.get(_p, 0) + _s[1] + _u - 1) // _u * _u
+    del SCRATCH[_n]
+for _p in _at:
+    SCRATCH[_p] = ("sbuf", [128, _at[_p]], _p[5:])
+
+DMAS = ["dsl", "dx", "dz0", "dz1", "dcl", "dwt", "dkp", "dyx", "dyl", "dyz0", "dyz1"]
+SEMAPHORES = ["eV", "eS", "eP", "eG", "sent"] + DMAS + ["aB%d" % q for q in range(1, 5)] + ["aW%d" % q for q in range(1, 5)] + ["ab%d" % t for t in range(1, VIS)]
+CY = 0.00083
+GA = 1.5
+
+
+def rank_program(g, core, T, topo):
+    rank = T.rank_of(core)
+    if rank is None:
+        return
+    build(g, rank, T, topo)
+
+
+def build(g, rank, T, topo, report=None):
+    ops = []
+    wr, rd, bank = {}, {}, {}
+    early = [0.0]
+
+    def ap(name, lo, hi, step=1, p=None):
+        buf, at = PLACE.get(name, (name, 0))
+        p = p or (0, 128)
+        if step == 1:
+            return T[buf][p[0]:p[1], at + lo:at + hi]
+        return T[buf][p[0]:p[1], at + lo:at + hi:step]
+
+    def B(name, lo=0, hi=None, step=1, p=None):
+        if hi is None:
+            hi = LOGICAL[name][1][1]
+        return (name, lo, hi, ap(name, lo, hi, step, p), (hi - lo + step - 1) // step)
+
+    def add(eng, call, outs, ins, cost, sem=None, amt=1, after=(), lat=0.06):
+        i = len(ops)
+        deps = {}
+
+        def dep(j, wait):
+            if j != i:
+                deps[j] = deps.get(j, False) or wait
+        for reg, isw in [(r, False) for r in ins] + [(r, True) for r in outs]:
+            name, lo, hi = reg[0], reg[1], reg[2]
+            psum = name[:2] == "pb"
+            for (a, b, j) in wr.get(name, []):
+                if a < hi and lo < b:
+                    dep(j, not (psum and eng == "P" and ops[j]["eng"] == "P"))
+            if isw:
+                for (a, b, j) in rd.get(name, []):
+                    if a < hi and lo < b:
+                        dep(j, True)
+            if psum:
+                e, run, prev = bank.setdefault(name, (eng, [], []))
+                if e != eng:
+                    e, run, prev = bank[name] = (eng, [], run)
+                for j in prev:
+                    dep(j, True)
+                if eng == "P" and run:
+                    dep(run[-1], False)
+                if i not in run:
+                    run.append(i)
+        for j in after:
+            dep(j, True)
+        for reg in ins:
+            rd.setdefault(reg[0], []).append((reg[1], reg[2], i))
+        for reg in outs:
+            name, lo, hi = reg[0], reg[1], reg[2]
+            if reg[4] == hi - lo:
+                wr[name] = [x for x in wr.get(name, []) if not (lo <= x[0] and x[1] <= hi)]
+                rd[name] = [x for x in rd.get(name, []) if not (lo <= x[0] and x[1] <= hi)]
+            wr.setdefault(name, []).append((lo, hi, i))
+        ops.append({"eng": eng, "call": call, "deps": deps, "cost": cost, "sem": sem, "amt": amt, "lat": lat, "early": early[0]})
+        return i
+
+    def two(*rs):
+        return all(LOGICAL[r[0]][2] in ("bfloat16", "uint16") for r in rs)
+
+    def cyc(n):
+        return 0.02 + max(64, n) * CY
+
+    def cp(o, i):
+        return add("V", lambda: g.vector.tensor_copy(o[3], i[3]), [o], [i], cyc(i[4] * (0.5 if two(o, i) else 1)))
+
+    def tt(o, a, b, op):
+        n = a[4] if (a[0][:2] == "pb" or b[0][:2] == "pb") else 2 * a[4]
+        return add("V", lambda: g.vector.tensor_tensor(o[3], a[3], b[3], op), [o], [a, b], cyc(n))
+
+    def tsc(o, i, s1, s2, op0, op1=None):
+        ins = [i] + [s for s in (s1, s2) if isinstance(s, tuple)]
+        v1 = s1[3] if isinstance(s1, tuple) else s1
+        v2 = s2[3] if isinstance(s2, tuple) else s2
+        if op1 is None:
+            f = lambda: g.vector.tensor_scalar(o[3], i[3], v1, None, op0)
+        else:
+            f = lambda: g.vector.tensor_scalar(o[3], i[3], v1, v2, op0, op1)
+        return add("V", f, [o], ins, cyc(i[4] * (0.5 if two(o, i) else 1)))
+
+    def gtt(o, w, off, b, op):
+        return add("V", lambda: g.vector.tensor_tensor(o[3], w[3].indirect(off[3]), b[3], op), [o], [w, off, b], 0.05 + o[4] * GA * CY)
+
+    def gcp(o, w, off):
+        return add("V", lambda: g.vector.tensor_copy(o[3], w[3].indirect(off[3])), [o], [w, off], 0.05 + o[4] * GA * CY)
+
+    def scat(w, off, i):
+        return add("V", lambda: g.vector.tensor_copy(w[3].indirect(off[3]), i[3]), [(w[0], w[1], w[2], w[3], -1)], [off, i], 0.05 + i[4] * 3 * CY)
+
+    def mem(o, c):
+        return add("V", lambda: g.vector.memset(o[3], c), [o], [], cyc(o[4] * 0.5))
+
+    def act(o, i, f, bias=None, scale=1.0):
+        ins = [i] + [s for s in (bias, scale) if isinstance(s, tuple)]
+        sc = scale[3] if isinstance(scale, tuple) else scale
+        if bias is None:
+            h = lambda: g.scalar.activation(o[3], i[3], f, scale=sc)
+        else:
+            h = lambda: g.scalar.activation(o[3], i[3], f, bias=bias[3], scale=sc)
+        return add("S", h, [o], ins, 0.05 + max(64, i[4]) * CY)
+
+    def gact(o, w, off):
+        return add("S", lambda: g.scalar.activation(o[3], w[3].indirect(off[3]), AF.Copy), [o], [w, off], 0.065 + o[4] * GA * CY)
+
+    def mm(o, l, r, start, stop, f32=False):
+        return add("P", lambda: g.tensor.matmul(o[3], l[3], r[3], start, stop), [o], [l, r], max(64, r[4]) * 0.00042 * (4 if f32 else 1))
+
+    def rows(o, lh, src, lo, width, extra=None):
+        for r in range(16):
+            mm(o, B(lh, 15 - r, 143 - r), B(src, lo + r, lo + width, 16), r == 0, r == 15 and extra is None)
+        if extra is not None:
+            for x, (l, r) in enumerate(extra):
+                mm(o, l, r, False, x == len(extra) - 1)
+
+    def dma(q, o, i, sem, us):
+        eng = {"Y": g.sync, "S": g.scalar}[q]
+        outs = [o] if o[0] in LOGICAL else []
+        ins = [i] if i[0] in LOGICAL else []
+        j = add(q, lambda: eng.dma_start(o[3], i[3]), outs, ins, 0.06, sem=sem, amt=16, lat=us)
+        ops[j]["dma"] = True
+        return j
+
+    def D(name, lo, hi, whole=False):
+        return (name, lo, hi, T[name][:] if whole else T[name][:, lo:hi], hi - lo)
+
+    sent = [0]
+
+    def send(name, o, i, dst, sem, us, after=None):
+        src_core, dst_core = T.cores[rank], T.cores[dst]
+        m = topo.mask(src_core, dst_core)
+        n = len(topo.engines(src_core, dst_core))
+        rid, pid, _se = topo.addr(dst_core)
+        j = add("G", lambda: g.remote_dma(out_ap=o[3], in_ap=i[3], remote_sem=T.sem[sem], local_sem=T.sem.sent, pid=pid, routing_id=rid, dma_engine_mask=m),
+                [], [i], 0.5, sem="-", amt=0)
+        sent[0] += n
+        k = add("R" + sem, None, [o], [], 0.0, sem=sem, amt=len(topo.engines(src_core, dst_core)), lat=us)
+        ops[k]["deps"][j] = False
+        return k
+
+    def asel(o, i, pat, cop, fill, base, cmul):
+        n = o[4]
+        return add("G", lambda: g.affine_select(o[3], i[3], pat, cop, fill, base, cmul), [o], [i], 0.17 + 2 * n * CY)
+
+    def iota(o, pat, base, cmul, flag=False):
+        if flag:
+            f = lambda: g.iota(o[3], pat, base, cmul, allow_small_or_imprecise_dtypes=True)
+        else:
+            f = lambda: g.iota(o[3], pat, base, cmul)
+        return add("G", f, [o], [], 0.13 + 2 * o[4] * CY)
+
+    hb = lambda n, h, lo=0, hi=None, step=1: B("%s_%d" % (n, h), lo, hi, step)
+    smb = lambda h: "pb%d" % h
+    if H == 1:
+        cnt_regs = lambda h: [("pb1", 0, 288), ("pb2", 288, 576)]
+        scb, prb, umb, rot = (lambda h: "pb1"), (lambda h: "pb2"), (lambda h: "pb2"), [["pb3", "pb4", "pb5", "pb6", "pb7"]]
+    else:
+        cnt_regs = lambda h: [("pb%d" % (2 + h), 0, 288)]
+        scb, prb, umb, rot = (lambda h: "pb%d" % (2 + h)), (lambda h: "pb%d" % (2 + h)), (lambda h: "pb%d" % (2 + h)), [["pb4", "pb5"], ["pb6", "pb7"]]
+    P0 = 288 + L
+    if H == 1:
+        P0 = 288
+    rc = [0, 0]
+
+    def rb(h):
+        rc[h] += 1
+        return rot[h][rc[h] % len(rot[h])]
+
+    E = lambda r: B("SL", 15 - r, 143 - r)
+
+    dma("Y", B("sln"), D("sl", 0, LA, True), "dsl", 2.2)
+    dma("S", B("CL"), D("cl", 0, V, True), "dcl", 6.0)
+    dma("Y", B("X", 0, W), D("x0", 0, W, True), "dx", 5.0)
+    dma("Y", B("kpi"), D("kp", 0, 1, True), "dkp", 2.2)
+    dma("Y", B("wti"), D("wt", 0, 1, True), "dwt", 2.2)
+    for h in range(H):
+        dma("Y", hb("Ca", h, 3 * L, 4 * L), D("z0", h * L, (h + 1) * L), "dz%d" % h, 2.2)
+
+    mem(B("spk", 0, 144), 0.0)
+    mem(B("cmk0"), 0.0)
+    mem(B("cmk1"), 0.0)
+    mem(B("ones", 0, 128), 1.0)
+    mem(B("spk", 15, 144, 16), 1.0)
+    for a in range(4):
+        mem(B("cmk0", 32 * a, 32 * a + 16), 1.0)
+        mem(B("cmk1", 32 * a + 16, 32 * a + 32), 1.0)
+    mem(B("neg"), -512.0)
+    iota(B("pc"), [[0, 1]], 0, 1)
+    for g2 in range(2):
+        for c2 in range(2):
+            asel(B("PM%d%d" % (g2, c2)), B("cmk%d" % g2), [[-1, 128]], OP.is_equal, 0.0, 16 * (g2 - c2), 1)
+    iota(B("g16"), [[16, 12]], 0, 0)
+    asel(B("BOa"), B("ones", 0, 128), [[-16, 8], [0, 16]], OP.is_ge, 0.0, 0, 1)
+    asel(B("BO"), B("BOa"), [[16, 8], [0, 16]], OP.is_ge, 0.0, 15, -1)
+    asel(B("Q16", 0, 128, 1, (0, 16)), B("ones", 0, 128, 1, (0, 16)), [[0, 8], [-1, 16]], OP.is_equal, 0.0, 0, 1)
+    asel(B("I"), B("ones", 0, 128), [[-1, 128]], OP.is_equal, 0.0, 0, 1)
+    asel(B("SLa"), B("spk"), [[-16, 9], [0, 16]], OP.is_ge, 0.0, 0, 1)
+    asel(B("SL"), B("SLa"), [[16, 9], [0, 16]], OP.is_ge, 0.0, 15, -1)
+    asel(B("Tri"), B("BO"), [[1, 128]], OP.is_ge, 0.0, 0, -1)
+    iota(B("KIL"), [[L, 16], [0, C]], 0, 0, True)
+    asel(B("R"), B("neg"), [[-1, 16], [-16, 8], [0, 16]], OP.is_equal, 0.0, 0, 1)
+    mm(B("pb7", 0, 128), B("Q16", 0, 128, 1, (0, 16)), B("Q16", 0, 128, 1, (0, 16)), True, True)
+    cp(B("GR"), B("pb7", 0, 128))
+    tsc(B("p15"), B("pc"), 15, None, OP.bitwise_and)
+    cp(B("p15f"), B("p15"))
+    tsc(B("kempty"), B("p15f"), -1.0, float(ZB + 16), OP.mult, OP.add)
+    cp(B("sad"), B("sln"))
+    tsc(B("sae"), B("sad"), 0.0, B("kempty"), OP.is_lt, OP.mult)
+    tt(B("T1"), B("sad"), B("sae"), OP.add)
+    add("V", lambda: g.vector.transpose(B("T2")[3], B("T1")[3]), [B("T2")], [B("T1")], cyc(192))
+    for g2 in range(2):
+        for b in range(6):
+            hh, b1 = b // BH, b % BH
+            lo = g2 * 96 + hh * (96 // H) + b1
+            cp(B("T3", lo, g2 * 96 + (hh + 1) * (96 // H), BH), B("T2", 32 * b + 16 * g2, 32 * b + 16 * g2 + 16))
+    for c2 in range(2):
+        for g2 in range(2):
+            mm(B("pb6", c2 * 96, c2 * 96 + 96), B("PM%d%d" % (g2, c2)), B("T3", g2 * 96, g2 * 96 + 96), g2 == 0, g2 == 1, True)
+    for h in range(H):
+        n = 96 // H
+        for c2 in range(2):
+            cp(hb("s", h, c2, 16 * C, 2), B("pb6", c2 * 96 + h * n, c2 * 96 + (h + 1) * n))
+        cp(hb("s16", h), hb("s", h))
+    mem(B("X", W, W + 16), 0.0)
+    for h in range(H):
+        mem(hb("Oa", h, 16 * L, 17 * L), 0.0)
+        mem(hb("Ob", h, 16 * L, 17 * L), 0.0)
+    cp(B("WK0", 0, 1), B("wti"))
+    cp(B("kpf"), B("kpi"))
+    tsc(B("kpd"), B("GR", 0, 16), B("kpf"), None, OP.mult)
+    mm(B("pb5", 0, 16), B("BO"), B("kpd"), True, True)
+    cp(B("WK0", 1, 17), B("pb5", 0, 16))
+    mem(B("WK0", 17, 24), 0.0)
+    for q in range(1, 5):
+        if q == 1:
+            send("b", B("BK1"), B("CL"), (rank - 1) % N, "aB1", 14.0)
+        send("w", B("WK%d" % q), B("WK0"), (rank - q) % N, "aW%d" % q, 4.0)
+    for q in range(2, 5):
+        send("b", B("BK%d" % q), B("CL"), (rank - q) % N, "aB%d" % q, 14.0 * q)
+    tsc(B("nI"), B("I"), -1.0, None, OP.mult)
+    for nm, v in (("I128", 128.0), ("I3", -3.0 * L), ("I2", -2.0 * L), ("I1", -1.0 * L)):
+        tsc(B(nm), B("I"), v, None, OP.mult)
+    tsc(B("SLL"), B("SL"), L / 2.0, None, OP.mult)
+    tsc(B("SLh"), B("SL"), 0.5, None, OP.mult)
+    mem(B("c8L"), 8.0 * L)
+    mem(B("c8L", C, 2 * C), 0.0)
+    mem(B("p15t"), 0)
+    tsc(B("LI"), B("p15t"), B("p15f"), None, OP.add)
+    tt(B("LI"), B("LI"), B("g16"), OP.add)
+    tsc(B("recb"), B("LI"), 16.0, None, OP.mult)
+    for nm, w in (("TW", W3), ("TK", C)):
+        tsc(B("q12"), B("LI"), 1.0 / w, -0.5 + 0.5 / w, OP.mult, OP.add)
+        tsc(B("e12"), B("q12"), float(-w), None, OP.mult)
+        tt(B("q12"), B("e12"), B("LI"), OP.add)
+        cp(B(nm), B("q12"))
+    for j in range(3):
+        cp(B("LI3f", j * C, (j + 1) * C), B("LI", 0, C))
+        cp(B("LI3b", j * C, (j + 1) * C), B("LI", 0, C))
+    cp(B("LIb"), B("LI", 0, C))
+    mem(B("c3L"), 3.0 * L)
+    tsc(B("thrn"), B("p15f"), float(16 - SN * KB) - 0.5, -3.0, OP.is_ge, OP.mult)
+    tsc(B("thrn"), B("thrn"), 12.5, None, OP.add)
+    tsc(B("thrc"), B("p15f"), M0 - 0.5, 8.0, OP.is_ge, OP.mult)
+    tsc(B("thrc"), B("thrc"), -7.5, None, OP.add)
+    for j in range(3):
+        mem(B("cols", j, j + 1), j + 0.5)
+    for t in range(VIS):
+        mem(B("cols", 3 + t, 4 + t), 97.0 * t)
+    mem(B("B0"), 0)
+    tsc(B("SW0"), B("SL"), B("WK0", 0, 1), None, OP.mult)
+    for q in range(1, 5):
+        tsc(B("SW%d" % q), B("SL"), B("WK%d" % q, 0, 1), None, OP.mult)
+    half = B("cols", 0, 1)
+    Ob = lambda t, h: "%s_%d" % ("Oa" if t % 2 == 0 else "Ob", h)
+    Cb = lambda t, h: "%s_%d" % ("Ca" if t % 2 == 0 else "Cb", h)
+    TK = lambda n: B("TK", 0, n)
+
+    def gather(t, h):
+        last = {}
+        for b in range(NB):
+            o = B(Ob(t, h), 384 * b, 384 * b + 384)
+            off = hb("s16", h, KB * C * b, KB * C * (b + 1))
+            if b in GV[min(t, 1)]:
+                j = gcp(o, B("X"), off)
+            else:
+                j = gact(o, B("X"), off)
+            e = ops[j]["eng"]
+            if e in last:
+                ops[j]["deps"].setdefault(last[e], False)
+            last[e] = j
+
+    def tile(h, src, lo):
+        for a in range(KB):
+            mm(B(smb(h), a * L, (a + 1) * L), B("I"), B(src, lo, lo + L), True, True)
+        return B(smb(h), 0, 384)
+
+    def diff(t, h, b, src, lo):
+        bk = rb(h)
+        mm(B(bk, 0, 384), B("I"), B(Ob(t, h), 384 * b, 384 * b + 384), True, False)
+        for a in range(KB):
+            mm(B(bk, a * L, (a + 1) * L), B("nI"), B(src, lo, lo + L), False, a == KB - 1)
+        return B(bk, 0, 384)
+
+    def test(t, h, src, lo, opv, fS, scale, bias, ns):
+        z = tile(h, src, lo)
+        vb, sb = list(range(NB - ns)), list(range(NB - ns, NB))
+        ks = []
+        for x in range(max(len(vb), len(sb))):
+            for lst in (vb, sb):
+                if x < len(lst):
+                    b = lst[x]
+                    o = hb("cmp", h, 384 * b, 384 * b + 384)
+                    if lst is vb:
+                        tt(o, B(Ob(t, h), 384 * b, 384 * b + 384), z, opv)
+                    else:
+                        act(o, diff(t, h, b, src, lo), fS, bias, scale)
+                    ks += range(KB * b, KB * b + KB)
+        cnt = B(scb(h), 288, 288 + L)
+        for x, k in enumerate(ks):
+            mm(cnt, E(k), hb("cmp", h, k * L, (k + 1) * L), x == 0, x == 15)
+        return cnt
+
+    def opened(t, h):
+        zc = Cb(t, h)
+        cnt = test(t, h, zc, 3 * L, OP.is_gt, AF.Relu, 1.0, None, SO)
+        act(hb("op", h), cnt, AF.Sign)
+        pr = B(prb(h), P0, P0 + L)
+        mm(pr, B("Tri"), hb("op", h), True, True)
+        pv = B(smb(h), 0, L)
+        mm(pv, B("Tri"), hb("op", h), True, True)
+        for j in (0, 2):
+            act(hb("le", h, j * L, (j + 1) * L), pr, AF.Sign, B("cols", j, j + 1), -1.0)
+        tsc(hb("le", h, L, 2 * L), pv, 1.5, 2.0, OP.is_le, OP.mult)
+        o = B(smb(h), 384, 384 + W3)
+        rows(o, "SLL", "le_%d" % h, 0, 3 * L, ((B("I"), B("LI3b")), (B("I"), B("c8L"))))
+        cp(hb("off", h), o)
+        for j in range(3):
+            gtt(B(zc, j * L, (j + 1) * L), B(Ob(t, h), 0, 17 * L), hb("off", h, j * C, (j + 1) * C), B(zc, 3 * L, 4 * L), OP.min)
+        fe = lambda a: hb("fe", h, a * C, (a + 1) * C)
+        kl = hb("kL", h)
+        tt(kl, o, B("LI3f"), OP.subtract)
+        tsc(hb("pen", h), kl, 15.0 * L, A[t] - 8 - 15.0 * L, OP.max, OP.add)
+        m = lambda a, b: hb("mx", h, a * C, b * C)
+        tt(m(0, 8), hb("s", h, 0, 8 * C), hb("s", h, 8 * C, 16 * C), OP.max)
+        tt(m(8, 12), m(0, 4), m(4, 8), OP.max)
+        tt(m(12, 14), m(8, 10), m(10, 12), OP.max)
+        tt(m(14, 15), m(12, 13), m(13, 14), OP.max)
+        tsc(fe(0), m(14, 15), float(ZB), None, OP.is_ge)
+        tsc(fe(1), m(14, 15), -1.0 * L, float(L * (ZB + 15 - t)), OP.mult, OP.add)
+        tt(fe(2), fe(0), fe(1), OP.mult)
+        tsc(fe(3), fe(2), float(L * t), None, OP.add)
+
+    def hashes(t, h):
+        u = B(smb(h), 384, 384 + W3)
+        q = t + 1
+        rows(u, "SW%d" % q, Cb(t, h), 0, 3 * L)
+        cp(hb("ui", h), u)
+        tsc(hb("um", h), hb("ui", h), V - 1, None, OP.bitwise_and)
+        cp(hb("uf", h), hb("um", h))
+        tt(hb("sq", h), hb("um", h), hb("um", h), OP.mult)
+        tsc(hb("ba", h), hb("sq", h), 5, None, OP.arith_shift_right)
+
+    def clauses(t, h):
+        q = t + 1
+        cand = Cb(t, h)
+        regs = cnt_regs(h)
+        sg = [0]
+        order = []
+        nv, ns = M0, 16 - M0
+        vs, ss = list(range(M0)), list(range(M0, 16))
+        while vs or ss:
+            if ss and (not vs or (16 - M0 - len(ss)) * M0 <= (M0 - len(vs)) * (16 - M0)):
+                order.append(ss.pop(0))
+            else:
+                order.append(vs.pop(0))
+        for ch in range(16 // MG):
+            ms = order[ch * MG:(ch + 1) * MG]
+            lo = ch * MG * W3
+            for x, m in enumerate(ms):
+                act(hb("KU", h, lo + x * W3, lo + (x + 1) * W3), hb("uf", h), AF.Identity, B("cols", 3 + t, 4 + t), B("WK%d" % q, 1 + m, 2 + m))
+            r = lambda n: hb(n, h, lo, lo + MG * W3)
+            gtt(r("Hs"), hb("ba", h), B("TW", 0, 9), r("KU"), OP.add)
+            tsc(r("Hm"), r("Hs"), V - 1, None, OP.bitwise_and)
+            cp(r("ho"), r("Hm"))
+        for x, m in enumerate(order):
+            off = hb("ho", h, x * W3, (x + 1) * W3)
+            gm = hb("G", h, m * 3 * L, (m + 1) * 3 * L)
+            if m < M0:
+                gtt(gm, B("BK%d" % q), off, B(cand, 0, 3 * L), OP.is_le)
+            else:
+                s0 = (sg[0] % 8) * 3 * L
+                sg[0] += 1
+                gact(hb("SG", h, s0, s0 + 3 * L), B("BK%d" % q), off)
+                for lo in range(0, 3 * L, 288):
+                    bk = rb(h)
+                    mm(B(bk, 0, 288), B("I"), hb("SG", h, s0 + lo, s0 + lo + 288), True, False)
+                    mm(B(bk, 0, 288), B("nI"), B(cand, lo, lo + 288), False, True)
+                    act(hb("G", h, m * 3 * L + lo, m * 3 * L + lo + 288), B(bk, 0, 288), AF.Sign, half, -1.0)
+            for bk, lo, hi in regs:
+                mm(B(bk, 0, 288), E(m), hb("G", h, m * 3 * L + lo, m * 3 * L + hi), x == 0, x == 15)
+        for bk, lo, hi in regs:
+            act(hb("ge", h, lo, hi), B(bk, 0, 288), AF.Sign, B("thrc"))
+
+    def trials(t, h):
+        cn = B(smb(h), 384, 384 + W3)
+        rows(cn, "SLh", "ge_%d" % h, 0, 3 * L)
+        cm = lambda j: hb("cm", h, j * C, (j + 1) * C)
+        nj = lambda j: hb("nb", h, 2 * j * C, (2 * j + 1) * C)
+        tt(hb("cm", h), cn, hb("pen", h), OP.subtract)
+        bit = B("B0", h * C, (h + 1) * C) if t == 0 else B("bl%d" % t, h * C, (h + 1) * C)
+        for j in range(3):
+            if j == 0:
+                tt(nj(0), cm(0), bit, OP.is_ge)
+            else:
+                d = hb("cd", h, (j - 1) * C, j * C)
+                tt(d, cm(j), B(smb(h), 448, 448 + C), OP.subtract)
+                tt(nj(j), d, bit, OP.is_ge)
+            if j < 2 or t < VIS - 1:
+                pn = B(smb(h), 432, 432 + C)
+                mm(pn, B("GR"), nj(j), True, True)
+                if j < 2:
+                    for i in range(j + 1):
+                        mm(B(smb(h), 448, 448 + C), B("I128"), nj(i), i == 0, i == j)
+                pi = hb("bt", h, j * C, (j + 1) * C)
+                cp(pi, pn)
+                if j < 2:
+                    bit = hb("ci", h, (6 + j) * C, (7 + j) * C)
+                else:
+                    bit = B("bs%d" % (t + 1), h * C, (h + 1) * C)
+                tsc(bit, pi, 1, None, OP.bitwise_and)
+        bo = B(smb(h), 464, 464 + C)
+        mm(bo, B("I"), B("LIb"), True, False)
+        mm(bo, B("I"), B("c3L"), False, False)
+        for j in range(3):
+            mm(bo, B("I%d" % (3 - j)), nj(j), False, j == 2)
+        cp(hb("bo", h), bo)
+        gact(hb("M", h), B(Cb(t, h), 0, 4 * L), hb("bo", h))
+
+    def post(t, h):
+        nb = lambda j, a, b: hb("nb", h, (2 * j + a) * C, (2 * j + b) * C)
+        um = B(umb(h), 480, 480 + C)
+        rows(um, "SW0", "M_%d" % h, 0, L)
+        ni = lambda a: hb("ni", h, a * C, (a + 1) * C)
+        cp(ni(0), um)
+        tsc(ni(1), ni(0), 15, None, OP.bitwise_and)
+        tt(hb("nf", h), ni(1), B("recb", h * C, (h + 1) * C), OP.add)
+        cp(hb("n16", h), hb("nf", h))
+        scat(B("X"), hb("n16", h), hb("M", h))
+        for j in range(3):
+            tt(nb(j, 1, 2), nb(j, 0, 1), hb("kL", h, j * C, (j + 1) * C), OP.mult)
+        s2 = B(smb(h), 480, 480 + 2 * C)
+        for j in range(3):
+            mm(s2, B("I"), nb(j, 0, 2), j == 0, j == 2)
+        pu = lambda a: hb("pu", h, a * C, (a + 1) * C)
+        fe = hb("fe", h, 3 * C, 4 * C)
+        tt(pu(0), B(smb(h), 480, 480 + C), fe, OP.mult)
+        tt(pu(1), B(smb(h), 480 + C, 480 + 2 * C), pu(0), OP.subtract)
+        tt(pu(2), pu(1), fe, OP.add)
+        gtt(hb("eq", h), pu(2), TK(C), B("KIL"), OP.is_equal)
+        gtt(hb("dd", h), hb("nf", h), TK(C), hb("s", h), OP.subtract)
+        tt(hb("ed", h), hb("eq", h), hb("dd", h), OP.mult)
+        tt(hb("s", h), hb("s", h), hb("ed", h), OP.add)
+        if t < VIS - 1:
+            cp(hb("s16", h), hb("s", h))
+
+    def near(t, h):
+        cnt = test(t, h, "M_%d" % h, 0, OP.is_le, AF.Sign, -1.0, half, SN)
+        act(hb("nn", h), cnt, AF.Relu, B("thrn"), -1.0)
+        for b in range(NB):
+            bk = rb(h)
+            mm(B(bk, 0, 384), B("I"), B(Ob(t, h), 384 * b, 384 * b + 384), True, False)
+            for a in range(KB):
+                k = KB * b + a
+                mm(B(bk, a * L, (a + 1) * L), B("R", 128 * k, 128 * k + 128), hb("nn", h), False, a == KB - 1)
+            if b == 0:
+                act(hb("acc", h), B(bk, 0, 384), AF.Relu)
+            else:
+                tt(hb("acc", h), B(bk, 0, 384), hb("acc", h), OP.max)
+        if KB == 4:
+            tt(hb("fo", h), hb("acc", h, 0, 192), hb("acc", h, 192, 384), OP.max)
+            tt(hb("cc", h), hb("fo", h, 0, L), hb("fo", h, L, 2 * L), OP.max)
+        else:
+            tt(hb("cc", h), hb("acc", h, 0, L), hb("acc", h, L, 2 * L), OP.max)
+        tt(hb("cc", h), hb("cc", h), hb("M", h), OP.max)
+        uc = B(umb(h), 496, 496 + C)
+        rows(uc, "SW0", "cc_%d" % h, 0, L)
+        ci = lambda a: hb("ci", h, a * C, (a + 1) * C)
+        cp(ci(0), uc)
+        tsc(ci(1), ci(0), V - 1, None, OP.bitwise_and)
+        tt(ci(2), ci(1), ci(1), OP.mult)
+        tsc(ci(3), ci(1), B("WK0", 1, 2), 97.0 * t, OP.mult, OP.add)
+        tsc(ci(4), ci(2), 5, None, OP.arith_shift_right)
+        tt(ci(5), ci(3), ci(4), OP.add)
+        tsc(ci(0), ci(5), V - 1, None, OP.bitwise_and)
+        cp(hb("ch", h), ci(0))
+        gtt(hb("df", h), B("CL"), hb("ch", h), hb("cc", h), OP.subtract)
+        act(B(Cb(t + 1, h), 3 * L, 4 * L), hb("df", h), AF.Abs)
+
+    def visit_bits(t):
+        send("bit", B("bl%d" % (t + 1)), B("bs%d" % (t + 1)), (rank - 1) % N, "ab%d" % (t + 1), 4.0)
+
+    for h in range(H):
+        gather(0, h)
+    for t in range(VIS):
+        for h in range(H):
+            opened(t, h)
+            hashes(t, h)
+            clauses(t, h)
+            trials(t, h)
+        if t < VIS - 1:
+            visit_bits(t)
+        early[0] = LEAD
+        for h in range(H):
+            post(t, h)
+        early[0] = 0.0
+        for h in range(H):
+            near(t, h)
+        if t < VIS - 1:
+            for h in range(H):
+                gather(t + 1, h)
+    dma("Y", ("yx", 0, W, T.yx[:], W), B("X", 0, W), "dyx", 5.0)
+    for c2 in range(2):
+        for h in range(H):
+            n = 96 // H
+            cp(B("T3", c2 * 96 + h * n, c2 * 96 + (h + 1) * n), hb("s", h, c2, 16 * C, 2))
+    for g2 in range(2):
+        for c2 in range(2):
+            mm(B("pb3", g2 * 96, g2 * 96 + 96), B("PM%d%d" % (c2, g2)), B("T3", c2 * 96, c2 * 96 + 96), c2 == 0, c2 == 1, True)
+    for g2 in range(2):
+        for b in range(6):
+            hh, b1 = b // BH, b % BH
+            cp(B("T4", 32 * b + 16 * g2, 32 * b + 16 * g2 + 16), B("pb3", g2 * 96 + hh * (96 // H) + b1, g2 * 96 + (hh + 1) * (96 // H), BH))
+    add("V", lambda: g.vector.transpose(B("T5")[3], B("T4")[3]), [B("T5")], [B("T4")], cyc(192))
+    tsc(B("T6"), B("T5"), float(ZB), B("kempty"), OP.is_ge, OP.mult)
+    tt(B("T1"), B("T5"), B("T6"), OP.subtract)
+    dma("Y", ("yl", 0, LA, T.yl[:], LA), B("T1"), "dyl", 2.2)
+    for h in range(H):
+        dma("Y", ("yz", h * L, (h + 1) * L, T.yz[:, h * L:(h + 1) * L], L), B(Cb(VIS, h), 3 * L, 4 * L), "dyz%d" % h, 2.2)
+
+    order = schedule(ops)
+    emit(g, T, ops, order, sent[0])
+    if report is not None:
+        report.append((ops, order))
+
+
+def schedule(ops):
+    n = len(ops)
+    succ = [[] for _ in range(n)]
+    left = [0] * n
+    for i, o in enumerate(ops):
+        left[i] = len(o["deps"])
+        for j in o["deps"]:
+            succ[j].append(i)
+    tail = [0.0] * n
+    for i in range(n - 1, -1, -1):
+        o = ops[i]
+        tail[i] = o["cost"] + o["lat"] + max([tail[s] for s in succ[i]] + [0.0])
+    for i in range(n):
+        tail[i] += ops[i]["early"]
+    free, fin, est = {}, [0.0] * n, [0.0] * n
+    ready = [i for i in range(n) if left[i] == 0]
+    order = []
+    while ready:
+        st = [(max(free.get(ops[i]["eng"], 0.0), est[i]), i) for i in ready]
+        t0 = min(st)[0]
+        best = max((tail[i], -i) for s, i in st if s <= t0 + TOL)
+        i = -best[1]
+        o = ops[i]
+        s = max(free.get(o["eng"], 0.0), est[i])
+        o["start"] = s
+        free[o["eng"]] = s + o["cost"]
+        fin[i] = s + o["cost"] + o["lat"]
+        o["end"] = s + o["cost"]
+        order.append(i)
+        ready.remove(i)
+        for k in succ[i]:
+            e = fin[i] if (ops[k]["eng"] != o["eng"] or ops[k]["deps"][i]) else o["end"]
+            est[k] = max(est[k], e)
+            left[k] -= 1
+            if left[k] == 0:
+                ready.append(k)
+    return order
+
+
+def emit(g, T, ops, order, nsent):
+    queue = {"V": g.vector, "S": g.scalar, "P": g.tensor, "G": g, "Y": g.sync}
+    need = set()
+    for o in ops:
+        for j, w in o["deps"].items():
+            if w:
+                need.add(j)
+    total, mark, know, snap = {}, {}, {}, {}
+    for i in order:
+        o = ops[i]
+        e = o["eng"]
+        if e[0] == "R":
+            total[o["sem"]] = o["amt"]
+            mark[i] = (o["sem"], o["amt"])
+            snap[i] = {}
+            continue
+        k = know.setdefault(e, {})
+        want = {}
+        for j, w in o["deps"].items():
+            if w:
+                s, v = mark[j]
+                if k.get(s, 0) < v and want.get(s, (0, 0))[0] < v:
+                    want[s] = (v, j)
+        for s in list(want):
+            if any(s2 != s and snap[want[s2][1]].get(s, 0) >= want[s][0] for s2 in want):
+                del want[s]
+        for s, (v, j) in want.items():
+            queue[e].wait_ge(T.sem[s], v)
+            k[s] = max(k.get(s, 0), v)
+            for s2, v2 in snap[j].items():
+                k[s2] = max(k.get(s2, 0), v2)
+        ins = o["call"]()
+        if o["sem"] == "-":
+            continue
+        if o["sem"] is not None:
+            ins.then_inc(T.sem[o["sem"]], o["amt"])
+            total[o["sem"]] = o["amt"]
+            mark[i] = (o["sem"], o["amt"])
+        elif i in need:
+            s = "e" + e
+            ins.then_inc(T.sem[s], 1)
+            total[s] = total.get(s, 0) + 1
+            mark[i] = (s, total[s])
+        else:
+            continue
+        snap[i] = dict(k)
+    for s, v in total.items():
+        if know.get("G", {}).get(s, 0) < v:
+            g.wait_ge(T.sem[s], v)
+    g.wait_ge(T.sem.sent, nsent)

@@ -1,57 +1,49 @@
 from concourse.mybir import AluOpType as OP, ActivationFunctionType as AF
 
-H = 1
-N, LA, W, V, VIS, SUB = 8, 192, 3072, 4096, 4, 16
+N, LA, W, V, VIS = 8, 192, 3072, 4096, 4
 A = [6, 4, 4, 3]
 ZB = 3072
-L, C = LA // H, 12 // H
-W3 = 3 * C
-KB = 384 // L
-NB = 16 // KB
-SO = NB // 2
-SN = NB // 2
+L, C, W3 = 192, 12, 36
+NB = 8
+SO = 4
 M0 = 10
-MG = 144 // W3
-BH = 6 // H
-GV = (tuple(range(0, NB, 2)), ())
-TOL, LEAD = 0.02, 5.0
+GRP = ((0, 2), (2, 3))
+CHUNKS = (((0, 4), (4, 16)), ((0, 16),))
+GV = ((0, 2), ())
+TOL, LEAD, LAT = 0.02, 5.0, 0.15
+CY, GA = 0.00083, 1.5
 
 SCRATCH = {}
-for _n, _c, _d in (("X", W + 16, "bfloat16"), ("CL", V, "bfloat16"), ("ones", 128, "bfloat16"), ("neg", 2048, "bfloat16"), ("R", 2048, "bfloat16"), ("SLh", 144, "bfloat16"), ("c8L", W3, "bfloat16"),
-                   ("I", 128, "bfloat16"), ("nI", 128, "bfloat16"), ("I128", 128, "bfloat16"), ("I3", 128, "bfloat16"), ("I2", 128, "bfloat16"), ("I1", 128, "bfloat16"),
-                   ("spk", 144, "bfloat16"), ("SLa", 144, "bfloat16"), ("SL", 144, "bfloat16"), ("SLL", 144, "bfloat16"),
-                   ("BOa", 128, "bfloat16"), ("BO", 128, "bfloat16"), ("Tri", 128, "bfloat16"), ("Q16", 128, "bfloat16"), ("GR", 128, "bfloat16"),
-                   ("cmk0", 128, "float32"), ("cmk1", 128, "float32"), ("PM00", 128, "float32"), ("PM01", 128, "float32"), ("PM10", 128, "float32"), ("PM11", 128, "float32"),
-                   ("pc", 1, "int32"), ("p15", 1, "int32"), ("p15f", 1, "float32"), ("kempty", 1, "float32"), ("thrn", 1, "float32"), ("thrc", 1, "float32"), ("cols", 8, "float32"),
-                   ("g16", 12, "int32"), ("p15t", 12, "int32"), ("LI", 12, "int32"), ("e12", 12, "int32"), ("q12", 12, "int32"), ("TW", 12, "uint16"), ("TK", 12, "uint16"), ("recb", 12, "float32"),
-                   ("LI3f", W3, "float32"), ("LI3b", W3, "bfloat16"), ("LIb", C, "bfloat16"), ("c3L", C, "bfloat16"), ("KIL", 16 * C, "float32"),
-                   ("sln", LA, "int32"), ("sad", LA, "float32"), ("sae", LA, "float32"), ("T1", LA, "float32"), ("T2", LA, "float32"), ("T3", LA, "float32"), ("T4", LA, "float32"), ("T5", LA, "float32"), ("T6", LA, "float32"),
-                   ("wti", 1, "int32"), ("kpi", 1, "int32"), ("kpf", 1, "float32"), ("kpd", 16, "bfloat16"), ("WK0", 24, "float32"), ("B0", 12, "int32"), ("pint", 12, "int32")):
-    SCRATCH[_n] = ("sbuf", [128, _c], _d)
+for _t, _l in (
+        ("bfloat16", (("X", W + 16), ("CL", V), ("ones", 128), ("neg", 2048), ("R", 2048), ("SLh", 144), ("c8L", W3), ("I", 128), ("nI", 128),
+                      ("I64", 128), ("I3", 128), ("I2", 128), ("I1", 128), ("spk", 144), ("SLa", 144), ("SL", 144), ("SLL", 144), ("BOa", 128), ("BO", 128),
+                      ("Tri", 128), ("Q16", 128), ("GR", 128), ("GRh", 128), ("LI3b", W3), ("LIb", C), ("c3L", C), ("kpd", 16), ("DX", 576), ("DK", 576),
+                      ("Oa", 17 * L), ("Ob", 17 * L), ("Ca", 4 * L), ("Cb", 4 * L), ("cmp", 16 * L), ("op", L), ("le", 3 * L), ("G", 48 * L), ("SG", 16 * L),
+                      ("ge", 3 * L), ("nb", 6 * C), ("M", L), ("nn", L), ("acc", 768), ("fo", 384), ("cc", L), ("df", L))),
+        ("float32", (("cmk0", 128), ("cmk1", 128), ("PM00", 128), ("PM01", 128), ("PM10", 128), ("PM11", 128), ("p15f", 1), ("kempty", 1), ("thrn", 1),
+                     ("thrc", 1), ("cols", 1), ("recb", 12), ("LI3f", W3), ("KIL", L), ("sad", LA), ("sae", LA), ("T1", LA), ("T2", LA), ("T3", LA), ("T4", LA),
+                     ("T5", LA), ("T6", LA), ("kpf", 1), ("WK0", 24), ("B0", 12), ("kL", W3), ("pen", W3), ("KU", 576), ("cm", W3), ("cd", 2 * C), ("s", L),
+                     ("eq", L), ("dd", L), ("ed", L), ("mx", 15 * C), ("fe", 4 * C), ("pu", 3 * C), ("nf", C))),
+        ("int32", (("pc", 1), ("p15", 1), ("g16", 12), ("p15t", 12), ("LI", 12), ("e12", 12), ("q12", 12), ("sln", LA), ("wti", 1), ("kpi", 1),
+                   ("ui", W3), ("um", W3), ("sq", W3), ("ba", W3), ("Hs", 576), ("Hm", 576), ("bt", 3 * C), ("ci", 8 * C), ("ni", 2 * C))),
+        ("uint16", (("TW", 18), ("TK", 12), ("off", W3), ("ho", 576), ("bo", C), ("ch", C), ("s16", L), ("n16", C)))):
+    for _n, _c in _l:
+        SCRATCH[_n] = ("sbuf", [128, _c], _t)
 for _q in range(1, 5):
     SCRATCH["BK%d" % _q] = ("sbuf", [128, V], "bfloat16")
     SCRATCH["WK%d" % _q] = ("sbuf", [128, 24], "float32")
 for _q in range(5):
     SCRATCH["SW%d" % _q] = ("sbuf", [128, 144], "bfloat16")
+    SCRATCH["KX%d" % _q] = ("sbuf", [128, 576], "float32")
 for _t in range(1, VIS):
-    SCRATCH["bs%d" % _t] = ("sbuf", [128, 12], "int32")
-    SCRATCH["bl%d" % _t] = ("sbuf", [128, 12], "int32")
-for _h in range(H):
-    for _n, _c, _d in (("Oa", 17 * L, "bfloat16"), ("Ob", 17 * L, "bfloat16"), ("Ca", 4 * L, "bfloat16"), ("Cb", 4 * L, "bfloat16"), ("cmp", 16 * L, "bfloat16"),
-                       ("op", L, "bfloat16"), ("le", 3 * L, "bfloat16"), ("off", W3, "uint16"), ("kL", W3, "float32"), ("pen", W3, "float32"),
-                       ("ui", W3, "int32"), ("um", W3, "int32"), ("uf", W3, "float32"), ("sq", W3, "int32"), ("ba", W3, "int32"), ("KU", 16 * W3, "float32"), ("Hs", 16 * W3, "int32"), ("Hm", 16 * W3, "int32"), ("ho", 16 * W3, "uint16"),
-                       ("G", 48 * L, "bfloat16"), ("SG", 24 * L, "bfloat16"), ("ge", 3 * L, "bfloat16"), ("cm", W3, "float32"), ("cd", 2 * C, "float32"), ("nb", 6 * C, "bfloat16"), ("bt", 3 * C, "int32"), ("bo", C, "uint16"), ("M", L, "bfloat16"),
-                       ("nn", L, "bfloat16"), ("acc", 384, "bfloat16"), ("fo", 192, "bfloat16"), ("cc", L, "bfloat16"), ("df", L, "bfloat16"), ("ci", 8 * C, "int32"), ("ch", C, "uint16"),
-                       ("s", 16 * C, "float32"), ("s16", 16 * C, "uint16"), ("eq", 16 * C, "float32"), ("dd", 16 * C, "float32"), ("ed", 16 * C, "float32"),
-                       ("mx", 15 * C, "float32"), ("fe", 4 * C, "float32"), ("pu", 3 * C, "float32"), ("ni", 2 * C, "int32"), ("nf", C, "float32"), ("n16", C, "uint16")):
-        SCRATCH["%s_%d" % (_n, _h)] = ("sbuf", [128, _c], _d)
-for _b in range(8):
-    SCRATCH["pb%d" % _b] = ("psum", [128, 512], "float32")
-OWN = ("X", "CL", "sln", "wti", "kpi", "T1", "WK", "BK", "bs", "bl", "Ca", "Cb", "pb", "B0")
-LOGICAL, PLACE = dict(SCRATCH), {}
-_at = {}
+    SCRATCH["bs%d" % _t] = ("sbuf", [128, 12], "float32")
+    SCRATCH["bl%d" % _t] = ("sbuf", [128, 12], "float32")
+for _n, _c in (("pb0", 512), ("pbA", 1024), ("pbR0", 1024), ("pbR1", 1024)):
+    SCRATCH[_n] = ("psum", [128, _c], "float32")
+OWN = ("X", "CL", "sln", "wti", "kpi", "T1", "WK", "BK", "bs", "bl", "Ca", "Cb", "pb", "pbA", "pbR")
+LOGICAL, PLACE, _at = dict(SCRATCH), {}, {}
 for _n, (_w, _s, _d) in list(SCRATCH.items()):
-    if _n.split("_")[0].rstrip("0123456789") in OWN or _n in OWN:
+    if _n.rstrip("0123456789") in OWN or _n in OWN:
         continue
     _p = "pool_" + _d
     _u = 16 if _d in ("float32", "int32") else 32
@@ -61,10 +53,8 @@ for _n, (_w, _s, _d) in list(SCRATCH.items()):
 for _p in _at:
     SCRATCH[_p] = ("sbuf", [128, _at[_p]], _p[5:])
 
-DMAS = ["dsl", "dx", "dz0", "dz1", "dcl", "dwt", "dkp", "dyx", "dyl", "dyz0", "dyz1"]
-SEMAPHORES = ["eV", "eS", "eP", "eG", "sent"] + DMAS + ["aB%d" % q for q in range(1, 5)] + ["aW%d" % q for q in range(1, 5)] + ["ab%d" % t for t in range(1, VIS)]
-CY = 0.00083
-GA = 1.5
+SEMAPHORES = ["eV", "eS", "eP", "eG", "sent", "dsl", "dx", "dz", "dcl", "dcm", "dwt", "dkp", "dyx", "dyl", "dyz", "aC1", "aD2", "aD3", "aD4"]
+SEMAPHORES += ["aB%d" % q for q in range(1, 5)] + ["aW%d" % q for q in range(1, 5)] + ["ab%d" % t for t in range(1, VIS)]
 
 
 def rank_program(g, core, T, topo):
@@ -75,25 +65,17 @@ def rank_program(g, core, T, topo):
 
 
 def build(g, rank, T, topo, report=None):
-    ops = []
-    wr, rd, bank = {}, {}, {}
-    early = [0.0]
+    ops, wr, rd, bank, early = [], {}, {}, {}, [0.0]
 
-    def ap(name, lo, hi, step=1, p=None):
-        buf, at = PLACE.get(name, (name, 0))
-        p = p or (0, 128)
-        if step == 1:
-            return T[buf][p[0]:p[1], at + lo:at + hi]
-        return T[buf][p[0]:p[1], at + lo:at + hi:step]
-
-    def B(name, lo=0, hi=None, step=1, p=None):
+    def B(name, lo=0, hi=None, step=1, p=(0, 128)):
         if hi is None:
             hi = LOGICAL[name][1][1]
-        return (name, lo, hi, ap(name, lo, hi, step, p), (hi - lo + step - 1) // step)
+        buf, at = PLACE.get(name, (name, 0))
+        x = T[buf][p[0]:p[1], at + lo:at + hi] if step == 1 else T[buf][p[0]:p[1], at + lo:at + hi:step]
+        return (name, lo, hi, x, (hi - lo + step - 1) // step)
 
-    def add(eng, call, outs, ins, cost, sem=None, amt=1, after=(), lat=0.06):
-        i = len(ops)
-        deps = {}
+    def add(eng, call, outs, ins, cost, sem=None, amt=1, lat=LAT):
+        i, deps = len(ops), {}
 
         def dep(j, wait):
             if j != i:
@@ -109,17 +91,16 @@ def build(g, rank, T, topo, report=None):
                     if a < hi and lo < b:
                         dep(j, True)
             if psum:
-                e, run, prev = bank.setdefault(name, (eng, [], []))
-                if e != eng:
-                    e, run, prev = bank[name] = (eng, [], run)
-                for j in prev:
-                    dep(j, True)
-                if eng == "P" and run:
-                    dep(run[-1], False)
-                if i not in run:
-                    run.append(i)
-        for j in after:
-            dep(j, True)
+                for b in range(lo // 512, (hi - 1) // 512 + 1):
+                    e, run, prev = bank.setdefault((name, b), (eng, [], []))
+                    if e != eng:
+                        e, run, prev = bank[(name, b)] = (eng, [], run)
+                    for j in prev:
+                        dep(j, True)
+                    if eng == "P" and run:
+                        dep(run[-1], False)
+                    if i not in run:
+                        run.append(i)
         for reg in ins:
             rd.setdefault(reg[0], []).append((reg[1], reg[2], i))
         for reg in outs:
@@ -130,6 +111,9 @@ def build(g, rank, T, topo, report=None):
             wr.setdefault(name, []).append((lo, hi, i))
         ops.append({"eng": eng, "call": call, "deps": deps, "cost": cost, "sem": sem, "amt": amt, "lat": lat, "early": early[0]})
         return i
+
+    def order_after(i, j):
+        ops[i]["deps"].setdefault(j, False)
 
     def two(*rs):
         return all(LOGICAL[r[0]][2] in ("bfloat16", "uint16") for r in rs)
@@ -168,11 +152,10 @@ def build(g, rank, T, topo, report=None):
 
     def act(o, i, f, bias=None, scale=1.0):
         ins = [i] + [s for s in (bias, scale) if isinstance(s, tuple)]
-        sc = scale[3] if isinstance(scale, tuple) else scale
         if bias is None:
-            h = lambda: g.scalar.activation(o[3], i[3], f, scale=sc)
+            h = lambda: g.scalar.activation(o[3], i[3], f, scale=scale)
         else:
-            h = lambda: g.scalar.activation(o[3], i[3], f, bias=bias[3], scale=sc)
+            h = lambda: g.scalar.activation(o[3], i[3], f, bias=bias[3], scale=scale)
         return add("S", h, [o], ins, 0.05 + max(64, i[4]) * CY)
 
     def gact(o, w, off):
@@ -181,41 +164,36 @@ def build(g, rank, T, topo, report=None):
     def mm(o, l, r, start, stop, f32=False):
         return add("P", lambda: g.tensor.matmul(o[3], l[3], r[3], start, stop), [o], [l, r], max(64, r[4]) * 0.00042 * (4 if f32 else 1))
 
-    def rows(o, lh, src, lo, width, extra=None):
+    E = lambda r, nm="SL": B(nm, 15 - r, 143 - r)
+
+    def rows(o, nm, src, lo, width, extra=()):
         for r in range(16):
-            mm(o, B(lh, 15 - r, 143 - r), B(src, lo + r, lo + width, 16), r == 0, r == 15 and extra is None)
-        if extra is not None:
-            for x, (l, r) in enumerate(extra):
-                mm(o, l, r, False, x == len(extra) - 1)
+            mm(o, E(r, nm), B(src, lo + r, lo + width, 16), r == 0, r == 15 and not extra)
+        for x, (l, r) in enumerate(extra):
+            mm(o, l, r, False, x == len(extra) - 1)
 
     def dma(q, o, i, sem, us):
         eng = {"Y": g.sync, "S": g.scalar}[q]
-        outs = [o] if o[0] in LOGICAL else []
-        ins = [i] if i[0] in LOGICAL else []
-        j = add(q, lambda: eng.dma_start(o[3], i[3]), outs, ins, 0.06, sem=sem, amt=16, lat=us)
-        ops[j]["dma"] = True
-        return j
+        return add(q, lambda: eng.dma_start(o[3], i[3]), [o] if o[0] in LOGICAL else [], [i] if i[0] in LOGICAL else [], 0.06, sem=sem, amt=16, lat=us)
 
-    def D(name, lo, hi, whole=False):
-        return (name, lo, hi, T[name][:] if whole else T[name][:, lo:hi], hi - lo)
+    def D(name, lo, hi):
+        return (name, lo, hi, T[name][:, lo:hi] if hi - lo < T[name].shape[1] else T[name][:], hi - lo)
 
     sent = [0]
 
-    def send(name, o, i, dst, sem, us, after=None):
+    def send(o, i, dst, sem, us):
         src_core, dst_core = T.cores[rank], T.cores[dst]
-        m = topo.mask(src_core, dst_core)
-        n = len(topo.engines(src_core, dst_core))
+        m, n = topo.mask(src_core, dst_core), len(topo.engines(src_core, dst_core))
         rid, pid, _se = topo.addr(dst_core)
         j = add("G", lambda: g.remote_dma(out_ap=o[3], in_ap=i[3], remote_sem=T.sem[sem], local_sem=T.sem.sent, pid=pid, routing_id=rid, dma_engine_mask=m),
                 [], [i], 0.5, sem="-", amt=0)
         sent[0] += n
-        k = add("R" + sem, None, [o], [], 0.0, sem=sem, amt=len(topo.engines(src_core, dst_core)), lat=us)
+        k = add("R" + sem, None, [o], [], 0.0, sem=sem, amt=n, lat=us)
         ops[k]["deps"][j] = False
-        return k
+        return j
 
     def asel(o, i, pat, cop, fill, base, cmul):
-        n = o[4]
-        return add("G", lambda: g.affine_select(o[3], i[3], pat, cop, fill, base, cmul), [o], [i], 0.17 + 2 * n * CY)
+        return add("G", lambda: g.affine_select(o[3], i[3], pat, cop, fill, base, cmul), [o], [i], 0.17 + 2 * o[4] * CY)
 
     def iota(o, pat, base, cmul, flag=False):
         if flag:
@@ -224,37 +202,33 @@ def build(g, rank, T, topo, report=None):
             f = lambda: g.iota(o[3], pat, base, cmul)
         return add("G", f, [o], [], 0.13 + 2 * o[4] * CY)
 
-    hb = lambda n, h, lo=0, hi=None, step=1: B("%s_%d" % (n, h), lo, hi, step)
-    smb = lambda h: "pb%d" % h
-    if H == 1:
-        cnt_regs = lambda h: [("pb1", 0, 288), ("pb2", 288, 576)]
-        scb, prb, umb, rot = (lambda h: "pb1"), (lambda h: "pb2"), (lambda h: "pb2"), [["pb3", "pb4", "pb5", "pb6", "pb7"]]
-    else:
-        cnt_regs = lambda h: [("pb%d" % (2 + h), 0, 288)]
-        scb, prb, umb, rot = (lambda h: "pb%d" % (2 + h)), (lambda h: "pb%d" % (2 + h)), (lambda h: "pb%d" % (2 + h)), [["pb4", "pb5"], ["pb6", "pb7"]]
-    P0 = 288 + L
-    if H == 1:
-        P0 = 288
-    rc = [0, 0]
+    pairs = [0]
 
-    def rb(h):
-        rc[h] += 1
-        return rot[h][rc[h] % len(rot[h])]
+    def pair():
+        pairs[0] += 1
+        return "pbR%d" % (pairs[0] % 2)
 
-    E = lambda r: B("SL", 15 - r, 143 - r)
+    def clause_order():
+        order, vs, ss = [], list(range(M0)), list(range(M0, 16))
+        while vs or ss:
+            if ss and (not vs or (16 - M0 - len(ss)) * M0 <= (M0 - len(vs)) * (16 - M0)):
+                order.append(ss.pop(0))
+            else:
+                order.append(vs.pop(0))
+        return order
 
-    dma("Y", B("sln"), D("sl", 0, LA, True), "dsl", 2.2)
-    dma("S", B("CL"), D("cl", 0, V, True), "dcl", 6.0)
-    dma("Y", B("X", 0, W), D("x0", 0, W, True), "dx", 5.0)
-    dma("Y", B("kpi"), D("kp", 0, 1, True), "dkp", 2.2)
-    dma("Y", B("wti"), D("wt", 0, 1, True), "dwt", 2.2)
-    for h in range(H):
-        dma("Y", hb("Ca", h, 3 * L, 4 * L), D("z0", h * L, (h + 1) * L), "dz%d" % h, 2.2)
+    dma("Y", B("sln"), D("sl", 0, LA), "dsl", 2.2)
+    dma("S", B("CL", 0, V // 2), D("cl", 0, V // 2), "dcl", 4.0)
+    dma("S", B("CL", V // 2, V), D("cl", V // 2, V), "dcm", 6.0)
+    dma("Y", B("X", 0, W), D("x0", 0, W), "dx", 5.0)
+    dma("Y", B("kpi"), D("kp", 0, 1), "dkp", 2.2)
+    dma("Y", B("wti"), D("wt", 0, 1), "dwt", 2.2)
+    dma("Y", B("Ca", 3 * L, 4 * L), D("z0", 0, LA), "dz", 2.2)
 
     mem(B("spk", 0, 144), 0.0)
     mem(B("cmk0"), 0.0)
     mem(B("cmk1"), 0.0)
-    mem(B("ones", 0, 128), 1.0)
+    mem(B("ones"), 1.0)
     mem(B("spk", 15, 144, 16), 1.0)
     for a in range(4):
         mem(B("cmk0", 32 * a, 32 * a + 16), 1.0)
@@ -265,17 +239,17 @@ def build(g, rank, T, topo, report=None):
         for c2 in range(2):
             asel(B("PM%d%d" % (g2, c2)), B("cmk%d" % g2), [[-1, 128]], OP.is_equal, 0.0, 16 * (g2 - c2), 1)
     iota(B("g16"), [[16, 12]], 0, 0)
-    asel(B("BOa"), B("ones", 0, 128), [[-16, 8], [0, 16]], OP.is_ge, 0.0, 0, 1)
+    asel(B("BOa"), B("ones"), [[-16, 8], [0, 16]], OP.is_ge, 0.0, 0, 1)
     asel(B("BO"), B("BOa"), [[16, 8], [0, 16]], OP.is_ge, 0.0, 15, -1)
-    asel(B("Q16", 0, 128, 1, (0, 16)), B("ones", 0, 128, 1, (0, 16)), [[0, 8], [-1, 16]], OP.is_equal, 0.0, 0, 1)
-    asel(B("I"), B("ones", 0, 128), [[-1, 128]], OP.is_equal, 0.0, 0, 1)
+    low = (0, 16)
+    asel(B("Q16", 0, 128, 1, low), B("ones", 0, 128, 1, low), [[0, 8], [-1, 16]], OP.is_equal, 0.0, 0, 1)
+    asel(B("I"), B("ones"), [[-1, 128]], OP.is_equal, 0.0, 0, 1)
     asel(B("SLa"), B("spk"), [[-16, 9], [0, 16]], OP.is_ge, 0.0, 0, 1)
     asel(B("SL"), B("SLa"), [[16, 9], [0, 16]], OP.is_ge, 0.0, 15, -1)
     asel(B("Tri"), B("BO"), [[1, 128]], OP.is_ge, 0.0, 0, -1)
     iota(B("KIL"), [[L, 16], [0, C]], 0, 0, True)
-    asel(B("R"), B("neg"), [[-1, 16], [-16, 8], [0, 16]], OP.is_equal, 0.0, 0, 1)
-    mm(B("pb7", 0, 128), B("Q16", 0, 128, 1, (0, 16)), B("Q16", 0, 128, 1, (0, 16)), True, True)
-    cp(B("GR"), B("pb7", 0, 128))
+    mm(B("pbR1", 512, 640), B("Q16", 0, 128, 1, low), B("Q16", 0, 128, 1, low), True, True)
+    cp(B("GR"), B("pbR1", 512, 640))
     tsc(B("p15"), B("pc"), 15, None, OP.bitwise_and)
     cp(B("p15f"), B("p15"))
     tsc(B("kempty"), B("p15f"), -1.0, float(ZB + 16), OP.mult, OP.add)
@@ -285,138 +259,151 @@ def build(g, rank, T, topo, report=None):
     add("V", lambda: g.vector.transpose(B("T2")[3], B("T1")[3]), [B("T2")], [B("T1")], cyc(192))
     for g2 in range(2):
         for b in range(6):
-            hh, b1 = b // BH, b % BH
-            lo = g2 * 96 + hh * (96 // H) + b1
-            cp(B("T3", lo, g2 * 96 + (hh + 1) * (96 // H), BH), B("T2", 32 * b + 16 * g2, 32 * b + 16 * g2 + 16))
+            cp(B("T3", g2 * 96 + b, g2 * 96 + 96, 6), B("T2", 32 * b + 16 * g2, 32 * b + 16 * g2 + 16))
     for c2 in range(2):
         for g2 in range(2):
-            mm(B("pb6", c2 * 96, c2 * 96 + 96), B("PM%d%d" % (g2, c2)), B("T3", g2 * 96, g2 * 96 + 96), g2 == 0, g2 == 1, True)
-    for h in range(H):
-        n = 96 // H
-        for c2 in range(2):
-            cp(hb("s", h, c2, 16 * C, 2), B("pb6", c2 * 96 + h * n, c2 * 96 + (h + 1) * n))
-        cp(hb("s16", h), hb("s", h))
+            mm(B("pbR0", c2 * 96, c2 * 96 + 96), B("PM%d%d" % (g2, c2)), B("T3", g2 * 96, g2 * 96 + 96), g2 == 0, g2 == 1, True)
+    for c2 in range(2):
+        cp(B("s", c2, L, 2), B("pbR0", c2 * 96, c2 * 96 + 96))
+    cp(B("s16"), B("s"))
     mem(B("X", W, W + 16), 0.0)
-    for h in range(H):
-        mem(hb("Oa", h, 16 * L, 17 * L), 0.0)
-        mem(hb("Ob", h, 16 * L, 17 * L), 0.0)
+    mem(B("Oa", 16 * L, 17 * L), 0.0)
+    mem(B("Ob", 16 * L, 17 * L), 0.0)
     cp(B("WK0", 0, 1), B("wti"))
     cp(B("kpf"), B("kpi"))
     tsc(B("kpd"), B("GR", 0, 16), B("kpf"), None, OP.mult)
-    mm(B("pb5", 0, 16), B("BO"), B("kpd"), True, True)
-    cp(B("WK0", 1, 17), B("pb5", 0, 16))
-    mem(B("WK0", 17, 24), 0.0)
+    mm(B("pbR1", 0, 16), B("BO"), B("kpd"), True, True)
+    cp(B("WK0", 1, 17), B("pbR1", 0, 16))
+    cp(B("WK0", 17, 18), B("kpi"))
+    mem(B("WK0", 18, 24), 0.0)
+    send(B("BK1", 0, V // 2), B("CL", 0, V // 2), (rank - 1) % N, "aC1", 9.0)
+    send(B("BK1", V // 2, V), B("CL", V // 2, V), (rank - 1) % N, "aB1", 12.0)
     for q in range(1, 5):
-        if q == 1:
-            send("b", B("BK1"), B("CL"), (rank - 1) % N, "aB1", 14.0)
-        send("w", B("WK%d" % q), B("WK0"), (rank - q) % N, "aW%d" % q, 4.0)
-    for q in range(2, 5):
-        send("b", B("BK%d" % q), B("CL"), (rank - q) % N, "aB%d" % q, 14.0 * q)
+        last = send(B("WK%d" % q), B("WK0"), (rank - q) % N, "aW%d" % q, 4.0)
+    order_after(asel(B("R"), B("neg"), [[-1, 16], [-16, 8], [0, 16]], OP.is_equal, 0.0, 0, 1), last)
+
+    def book(q):
+        x = 97 * (q - 1)
+        a = send(B("BK%d" % q, 0, V - x), B("CL", x, V), (rank - q) % N, "aB%d" % q, 14.0)
+        return a, send(B("BK%d" % q, V - x, V), B("CL", 0, x), (rank - q) % N, "aD%d" % q, 14.0)
+
+    book(2)
     tsc(B("nI"), B("I"), -1.0, None, OP.mult)
-    for nm, v in (("I128", 128.0), ("I3", -3.0 * L), ("I2", -2.0 * L), ("I1", -1.0 * L)):
+    tsc(B("GRh"), B("GR"), -0.5, None, OP.mult)
+    for nm, v in (("I64", -64.0), ("I3", -3.0 * L), ("I2", -2.0 * L), ("I1", -1.0 * L)):
         tsc(B(nm), B("I"), v, None, OP.mult)
     tsc(B("SLL"), B("SL"), L / 2.0, None, OP.mult)
-    tsc(B("SLh"), B("SL"), 0.5, None, OP.mult)
+    tsc(B("SLh"), B("SL"), 0.25, None, OP.mult)
     mem(B("c8L"), 8.0 * L)
-    mem(B("c8L", C, 2 * C), 0.0)
+    mem(B("c8L", C, 3 * C), 0.0)
     mem(B("p15t"), 0)
     tsc(B("LI"), B("p15t"), B("p15f"), None, OP.add)
     tt(B("LI"), B("LI"), B("g16"), OP.add)
     tsc(B("recb"), B("LI"), 16.0, None, OP.mult)
-    for nm, w in (("TW", W3), ("TK", C)):
+    for nm, w in (("TW", 2 * C), ("TK", C)):
         tsc(B("q12"), B("LI"), 1.0 / w, -0.5 + 0.5 / w, OP.mult, OP.add)
         tsc(B("e12"), B("q12"), float(-w), None, OP.mult)
         tt(B("q12"), B("e12"), B("LI"), OP.add)
-        cp(B(nm), B("q12"))
+        cp(B(nm, 0, 12), B("q12"))
+        if nm == "TW":
+            cp(B(nm, 12, 18), B("q12", 0, 6))
     for j in range(3):
-        cp(B("LI3f", j * C, (j + 1) * C), B("LI", 0, C))
-        cp(B("LI3b", j * C, (j + 1) * C), B("LI", 0, C))
-    cp(B("LIb"), B("LI", 0, C))
+        cp(B("LI3f", j * C, (j + 1) * C), B("LI"))
+        cp(B("LI3b", j * C, (j + 1) * C), B("LI"))
+    cp(B("LIb"), B("LI"))
     mem(B("c3L"), 3.0 * L)
-    tsc(B("thrn"), B("p15f"), float(16 - SN * KB) - 0.5, -3.0, OP.is_ge, OP.mult)
+    tsc(B("thrn"), B("p15f"), float(16 - 2 * SO) - 0.5, -3.0, OP.is_ge, OP.mult)
     tsc(B("thrn"), B("thrn"), 12.5, None, OP.add)
     tsc(B("thrc"), B("p15f"), M0 - 0.5, 8.0, OP.is_ge, OP.mult)
     tsc(B("thrc"), B("thrc"), -7.5, None, OP.add)
-    for j in range(3):
-        mem(B("cols", j, j + 1), j + 0.5)
-    for t in range(VIS):
-        mem(B("cols", 3 + t, 4 + t), 97.0 * t)
-    mem(B("B0"), 0)
+    mem(B("cols"), 0.5)
+    mem(B("B0"), 0.0)
+    for a, b in GRP:
+        w = (b - a) * C
+        for x, m in enumerate(clause_order()):
+            lo = 16 * a * C + x * w
+            act(B("DX", lo, lo + w), B("LI3f", 0, w), AF.Identity, B("GR", m, m + 1), 0.0)
     tsc(B("SW0"), B("SL"), B("WK0", 0, 1), None, OP.mult)
-    for q in range(1, 5):
-        tsc(B("SW%d" % q), B("SL"), B("WK%d" % q, 0, 1), None, OP.mult)
-    half = B("cols", 0, 1)
-    Ob = lambda t, h: "%s_%d" % ("Oa" if t % 2 == 0 else "Ob", h)
-    Cb = lambda t, h: "%s_%d" % ("Ca" if t % 2 == 0 else "Cb", h)
-    TK = lambda n: B("TK", 0, n)
+    half = B("cols")
+    Ob = lambda t: "Oa" if t % 2 == 0 else "Ob"
+    Cb = lambda t: "Ca" if t % 2 == 0 else "Cb"
 
-    def gather(t, h):
+    def judge(q):
+        tsc(B("SW%d" % q), B("SL"), B("WK%d" % q, 0, 1), None, OP.mult)
+        tsc(B("DK"), B("DX"), B("WK%d" % q, 17, 18), None, OP.mult)
+        bk = pair()
+        for at, lo, hi in ((128, 0, 384), (512, 384, 576)):
+            mm(B(bk, at, at + hi - lo), B("BO"), B("DK", lo, hi), True, True)
+        act(B("KX%d" % q), B(bk, 128, 704), AF.Copy)
+
+    def gather(t):
         last = {}
-        for b in range(NB):
-            o = B(Ob(t, h), 384 * b, 384 * b + 384)
-            off = hb("s16", h, KB * C * b, KB * C * (b + 1))
-            if b in GV[min(t, 1)]:
-                j = gcp(o, B("X"), off)
-            else:
-                j = gact(o, B("X"), off)
+        for b in range(NB // 2):
+            o, off = B(Ob(t), 768 * b, 768 * b + 768), B("s16", 48 * b, 48 * b + 48)
+            j = gcp(o, B("X"), off) if b in GV[min(t, 1)] else gact(o, B("X"), off)
             e = ops[j]["eng"]
             if e in last:
-                ops[j]["deps"].setdefault(last[e], False)
+                order_after(j, last[e])
             last[e] = j
 
-    def tile(h, src, lo):
-        for a in range(KB):
-            mm(B(smb(h), a * L, (a + 1) * L), B("I"), B(src, lo, lo + L), True, True)
-        return B(smb(h), 0, 384)
-
-    def diff(t, h, b, src, lo):
-        bk = rb(h)
-        mm(B(bk, 0, 384), B("I"), B(Ob(t, h), 384 * b, 384 * b + 384), True, False)
-        for a in range(KB):
-            mm(B(bk, a * L, (a + 1) * L), B("nI"), B(src, lo, lo + L), False, a == KB - 1)
-        return B(bk, 0, 384)
-
-    def test(t, h, src, lo, opv, fS, scale, bias, ns):
-        z = tile(h, src, lo)
-        vb, sb = list(range(NB - ns)), list(range(NB - ns, NB))
-        ks = []
-        for x in range(max(len(vb), len(sb))):
-            for lst in (vb, sb):
-                if x < len(lst):
-                    b = lst[x]
-                    o = hb("cmp", h, 384 * b, 384 * b + 384)
-                    if lst is vb:
-                        tt(o, B(Ob(t, h), 384 * b, 384 * b + 384), z, opv)
-                    else:
-                        act(o, diff(t, h, b, src, lo), fS, bias, scale)
-                    ks += range(KB * b, KB * b + KB)
-        cnt = B(scb(h), 288, 288 + L)
+    def test(t, src, lo, opv, fS, scale, bias):
+        for a in range(2):
+            mm(B("pb0", a * L, (a + 1) * L), B("I"), B(src, lo, lo + L), True, True)
+        vb, sb, ks = list(range(NB - SO)), list(range(NB - SO, NB, 2)), []
+        for x, b in enumerate(vb):
+            tt(B("cmp", 384 * b, 384 * b + 384), B(Ob(t), 384 * b, 384 * b + 384), B("pb0", 0, 384), opv)
+            ks += [2 * b, 2 * b + 1]
+            if x % 2 == 1 and x // 2 < len(sb):
+                b = sb[x // 2]
+                bk = pair()
+                for y in range(2):
+                    at = 128 + 384 * y
+                    mm(B(bk, at, at + 384), B("I"), B(Ob(t), 384 * (b + y), 384 * (b + y) + 384), True, False)
+                    for a in range(2):
+                        mm(B(bk, at + a * L, at + (a + 1) * L), B("nI"), B(src, lo, lo + L), False, a == 1)
+                act(B("cmp", 384 * b, 384 * b + 768), B(bk, 128, 896), fS, bias, scale)
+                ks += range(2 * b, 2 * b + 4)
+        cnt = B("pbA", 0, L)
         for x, k in enumerate(ks):
-            mm(cnt, E(k), hb("cmp", h, k * L, (k + 1) * L), x == 0, x == 15)
+            mm(cnt, E(k), B("cmp", k * L, (k + 1) * L), x == 0, x == 15)
         return cnt
 
-    def opened(t, h):
-        zc = Cb(t, h)
-        cnt = test(t, h, zc, 3 * L, OP.is_gt, AF.Relu, 1.0, None, SO)
-        act(hb("op", h), cnt, AF.Sign)
-        pr = B(prb(h), P0, P0 + L)
-        mm(pr, B("Tri"), hb("op", h), True, True)
-        pv = B(smb(h), 0, L)
-        mm(pv, B("Tri"), hb("op", h), True, True)
-        for j in (0, 2):
-            act(hb("le", h, j * L, (j + 1) * L), pr, AF.Sign, B("cols", j, j + 1), -1.0)
-        tsc(hb("le", h, L, 2 * L), pv, 1.5, 2.0, OP.is_le, OP.mult)
-        o = B(smb(h), 384, 384 + W3)
-        rows(o, "SLL", "le_%d" % h, 0, 3 * L, ((B("I"), B("LI3b")), (B("I"), B("c8L"))))
-        cp(hb("off", h), o)
-        for j in range(3):
-            gtt(B(zc, j * L, (j + 1) * L), B(Ob(t, h), 0, 17 * L), hb("off", h, j * C, (j + 1) * C), B(zc, 3 * L, 4 * L), OP.min)
-        fe = lambda a: hb("fe", h, a * C, (a + 1) * C)
-        kl = hb("kL", h)
-        tt(kl, o, B("LI3f"), OP.subtract)
-        tsc(hb("pen", h), kl, 15.0 * L, A[t] - 8 - 15.0 * L, OP.max, OP.add)
-        m = lambda a, b: hb("mx", h, a * C, b * C)
-        tt(m(0, 8), hb("s", h, 0, 8 * C), hb("s", h, 8 * C, 16 * C), OP.max)
+    def opened(t):
+        cnt = test(t, Cb(t), 3 * L, OP.is_gt, AF.Relu, 1.0, None)
+        act(B("op"), cnt, AF.Sign)
+        pr, pv = B("pbA", 800, 800 + L), B("pb0", 0, L)
+        mm(pr, B("Tri"), B("op"), True, True)
+        mm(pv, B("Tri"), B("op"), True, True)
+        act(B("le", 0, L), pr, AF.Sign, half, -1.0)
+        for j in (1, 2):
+            tsc(B("le", j * L, (j + 1) * L), pv, j + 0.5, 2.0, OP.is_le, OP.mult)
+
+    def small(u):
+        n = (GRP[u][1] - GRP[u][0]) * C
+        return B("pb0", 384, 384 + n) if u == 0 else B("pbA", 704, 704 + n)
+
+    def cands(t, u):
+        zc = Cb(t)
+        a, b = GRP[u]
+        sl = lambda n: B(n, a * C, b * C)
+        o = small(u)
+        rows(o, "SLL", "le", a * L, (b - a) * L, ((B("I"), sl("LI3b")), (B("I"), sl("c8L"))))
+        cp(sl("off"), o)
+        for j in range(a, b):
+            gtt(B(zc, j * L, (j + 1) * L), B(Ob(t), 0, 17 * L), B("off", j * C, (j + 1) * C), B(zc, 3 * L, 4 * L), OP.min)
+        tt(sl("kL"), o, sl("LI3f"), OP.subtract)
+        tsc(sl("pen"), sl("kL"), 15.0 * L, A[t] / 2.0 - 4 - 15.0 * L, OP.max, OP.add)
+        o = small(u)
+        rows(o, "SW%d" % (t + 1), zc, a * L, (b - a) * L)
+        cp(sl("ui"), o)
+        tsc(sl("um"), sl("ui"), V - 1, None, OP.bitwise_and)
+        tt(sl("sq"), sl("um"), sl("um"), OP.mult)
+        tsc(sl("ba"), sl("sq"), 5, None, OP.arith_shift_right)
+
+    def empties(t):
+        fe = lambda a: B("fe", a * C, (a + 1) * C)
+        m = lambda a, b: B("mx", a * C, b * C)
+        tt(m(0, 8), B("s", 0, 8 * C), B("s", 8 * C, 16 * C), OP.max)
         tt(m(8, 12), m(0, 4), m(4, 8), OP.max)
         tt(m(12, 14), m(8, 10), m(10, 12), OP.max)
         tt(m(14, 15), m(12, 13), m(13, 14), OP.max)
@@ -425,141 +412,134 @@ def build(g, rank, T, topo, report=None):
         tt(fe(2), fe(0), fe(1), OP.mult)
         tsc(fe(3), fe(2), float(L * t), None, OP.add)
 
-    def hashes(t, h):
-        u = B(smb(h), 384, 384 + W3)
-        q = t + 1
-        rows(u, "SW%d" % q, Cb(t, h), 0, 3 * L)
-        cp(hb("ui", h), u)
-        tsc(hb("um", h), hb("ui", h), V - 1, None, OP.bitwise_and)
-        cp(hb("uf", h), hb("um", h))
-        tt(hb("sq", h), hb("um", h), hb("um", h), OP.mult)
-        tsc(hb("ba", h), hb("sq", h), 5, None, OP.arith_shift_right)
-
-    def clauses(t, h):
-        q = t + 1
-        cand = Cb(t, h)
-        regs = cnt_regs(h)
-        sg = [0]
-        order = []
-        nv, ns = M0, 16 - M0
-        vs, ss = list(range(M0)), list(range(M0, 16))
-        while vs or ss:
-            if ss and (not vs or (16 - M0 - len(ss)) * M0 <= (M0 - len(vs)) * (16 - M0)):
-                order.append(ss.pop(0))
-            else:
-                order.append(vs.pop(0))
-        for ch in range(16 // MG):
-            ms = order[ch * MG:(ch + 1) * MG]
-            lo = ch * MG * W3
-            for x, m in enumerate(ms):
-                act(hb("KU", h, lo + x * W3, lo + (x + 1) * W3), hb("uf", h), AF.Identity, B("cols", 3 + t, 4 + t), B("WK%d" % q, 1 + m, 2 + m))
-            r = lambda n: hb(n, h, lo, lo + MG * W3)
-            gtt(r("Hs"), hb("ba", h), B("TW", 0, 9), r("KU"), OP.add)
+    def clauses(t, u):
+        q, cand, order = t + 1, Cb(t), clause_order()
+        a, b = GRP[u]
+        w, n = (b - a) * C, (b - a) * L
+        cnt = B("pbA", 512 * u, 512 * u + n)
+        last = None
+        for c0, c1 in CHUNKS[u]:
+            lo, hi = 16 * a * C + c0 * w, 16 * a * C + c1 * w
+            r = lambda nm: B(nm, lo, hi)
+            tw = B("TW" if b - a == 2 else "TK", 0, (c1 - c0) * w // 16)
+            j = gtt(r("KU"), B("um", a * C, b * C), tw, r("KX%d" % q), OP.mult)
+            if last is not None:
+                order_after(j, last)
+            gtt(r("Hs"), B("ba", a * C, b * C), tw, r("KU"), OP.add)
             tsc(r("Hm"), r("Hs"), V - 1, None, OP.bitwise_and)
-            cp(r("ho"), r("Hm"))
+            last = cp(r("ho"), r("Hm"))
+        sg = 0
         for x, m in enumerate(order):
-            off = hb("ho", h, x * W3, (x + 1) * W3)
-            gm = hb("G", h, m * 3 * L, (m + 1) * 3 * L)
+            off = B("ho", 16 * a * C + x * w, 16 * a * C + (x + 1) * w)
+            gm = B("G", m * 3 * L + a * L, m * 3 * L + b * L)
             if m < M0:
-                gtt(gm, B("BK%d" % q), off, B(cand, 0, 3 * L), OP.is_le)
+                gtt(gm, B("BK%d" % q), off, B(cand, a * L, b * L), OP.is_le)
             else:
-                s0 = (sg[0] % 8) * 3 * L
-                sg[0] += 1
-                gact(hb("SG", h, s0, s0 + 3 * L), B("BK%d" % q), off)
-                for lo in range(0, 3 * L, 288):
-                    bk = rb(h)
-                    mm(B(bk, 0, 288), B("I"), hb("SG", h, s0 + lo, s0 + lo + 288), True, False)
-                    mm(B(bk, 0, 288), B("nI"), B(cand, lo, lo + 288), False, True)
-                    act(hb("G", h, m * 3 * L + lo, m * 3 * L + lo + 288), B(bk, 0, 288), AF.Sign, half, -1.0)
-            for bk, lo, hi in regs:
-                mm(B(bk, 0, 288), E(m), hb("G", h, m * 3 * L + lo, m * 3 * L + hi), x == 0, x == 15)
-        for bk, lo, hi in regs:
-            act(hb("ge", h, lo, hi), B(bk, 0, 288), AF.Sign, B("thrc"))
+                s0 = (sg % 8) * 384
+                sg += 1
+                gact(B("SG", s0, s0 + n), B("BK%d" % q), off)
+                pairs[0] += 1
+                bk, at = "pbR%d" % (pairs[0] % 2), 512 * (pairs[0] // 2 % 2)
+                mm(B(bk, at, at + n), B("I"), B("SG", s0, s0 + n), True, False)
+                mm(B(bk, at, at + n), B("nI"), B(cand, a * L, b * L), False, True)
+                act(gm, B(bk, at, at + n), AF.Sign, half, -1.0)
+            mm(cnt, E(m), gm, x == 0, x == 15)
+        act(B("ge", a * L, b * L), cnt, AF.Sign, B("thrc"))
+        if u == 0 and t < VIS - 1:
+            judge(q + 1)
+        rows(small(u), "SLh", "ge", a * L, n)
 
-    def trials(t, h):
-        cn = B(smb(h), 384, 384 + W3)
-        rows(cn, "SLh", "ge_%d" % h, 0, 3 * L)
-        cm = lambda j: hb("cm", h, j * C, (j + 1) * C)
-        nj = lambda j: hb("nb", h, 2 * j * C, (2 * j + 1) * C)
-        tt(hb("cm", h), cn, hb("pen", h), OP.subtract)
-        bit = B("B0", h * C, (h + 1) * C) if t == 0 else B("bl%d" % t, h * C, (h + 1) * C)
-        for j in range(3):
-            if j == 0:
-                tt(nj(0), cm(0), bit, OP.is_ge)
-            else:
-                d = hb("cd", h, (j - 1) * C, j * C)
-                tt(d, cm(j), B(smb(h), 448, 448 + C), OP.subtract)
-                tt(nj(j), d, bit, OP.is_ge)
+    def trials(t, u):
+        nj = lambda j: B("nb", 2 * j * C, (2 * j + 1) * C)
+        a, b = GRP[u]
+        cn = small(u)
+        x = 0
+        if u == 0:
+            thr, x = B("cd", 0, C), C
+            tt(thr, B("pen", 0, C), B("B0") if t == 0 else B("bl%d" % t), OP.add)
+            tt(nj(0), B(cn[0], cn[1], cn[1] + C), thr, OP.is_ge)
+        tt(B("cm", a * C + x, b * C), B(cn[0], cn[1] + x, cn[2]), B("pen", a * C + x, b * C), OP.subtract)
+        pn, pd = B("pb0", 432, 432 + C), B("pb0", 448, 448 + C)
+        for j in range(a, b):
+            if j:
+                qn, d = B("bt", (j - 1) * C, j * C), B("cd", C, 2 * C)
+                tsc(qn, pn, 0.25, None, OP.add)
+                tt(d, B("cm", j * C, (j + 1) * C), pd, OP.add)
+                tt(nj(j), d, qn, OP.is_ge)
             if j < 2 or t < VIS - 1:
-                pn = B(smb(h), 432, 432 + C)
-                mm(pn, B("GR"), nj(j), True, True)
-                if j < 2:
-                    for i in range(j + 1):
-                        mm(B(smb(h), 448, 448 + C), B("I128"), nj(i), i == 0, i == j)
-                pi = hb("bt", h, j * C, (j + 1) * C)
-                cp(pi, pn)
-                if j < 2:
-                    bit = hb("ci", h, (6 + j) * C, (7 + j) * C)
-                else:
-                    bit = B("bs%d" % (t + 1), h * C, (h + 1) * C)
-                tsc(bit, pi, 1, None, OP.bitwise_and)
-        bo = B(smb(h), 464, 464 + C)
+                mm(pn, B("GRh"), nj(j), True, True)
+            if j < 2:
+                mm(pd, B("GRh"), nj(j), True, False)
+                for i in range(j + 1):
+                    mm(pd, B("I64"), nj(i), False, i == j)
+        if b < 3:
+            return
+        bo = B("pb0", 464, 464 + C)
         mm(bo, B("I"), B("LIb"), True, False)
         mm(bo, B("I"), B("c3L"), False, False)
         for j in range(3):
             mm(bo, B("I%d" % (3 - j)), nj(j), False, j == 2)
-        cp(hb("bo", h), bo)
-        gact(hb("M", h), B(Cb(t, h), 0, 4 * L), hb("bo", h))
+        x = cp(B("bo"), bo)
+        if t < VIS - 1:
+            pi, pj = B("bt", 2 * C, 3 * C), B("ci", 6 * C, 7 * C)
+            order_after(tsc(pi, pn, -2.0, None, OP.mult), x)
+            tsc(pj, pi, 1, None, OP.bitwise_and)
+            tsc(B("bs%d" % (t + 1)), pj, 0.5, None, OP.mult)
+        gact(B("M"), B(Cb(t), 0, 4 * L), B("bo"))
 
-    def post(t, h):
-        nb = lambda j, a, b: hb("nb", h, (2 * j + a) * C, (2 * j + b) * C)
-        um = B(umb(h), 480, 480 + C)
-        rows(um, "SW0", "M_%d" % h, 0, L)
-        ni = lambda a: hb("ni", h, a * C, (a + 1) * C)
+    def visit_bits(t):
+        k = send(B("bl%d" % (t + 1)), B("bs%d" % (t + 1)), (rank - 1) % N, "ab%d" % (t + 1), 4.0)
+        if t < 2:
+            for b in book(t + 3):
+                order_after(b, k)
+
+    def post(t):
+        nb = lambda j, a, b: B("nb", (2 * j + a) * C, (2 * j + b) * C)
+        um = B("pbA", 992, 992 + C)
+        rows(um, "SW0", "M", 0, L)
+        ni = lambda a: B("ni", a * C, (a + 1) * C)
         cp(ni(0), um)
         tsc(ni(1), ni(0), 15, None, OP.bitwise_and)
-        tt(hb("nf", h), ni(1), B("recb", h * C, (h + 1) * C), OP.add)
-        cp(hb("n16", h), hb("nf", h))
-        scat(B("X"), hb("n16", h), hb("M", h))
+        tt(B("nf"), ni(1), B("recb"), OP.add)
+        cp(B("n16"), B("nf"))
+        scat(B("X"), B("n16"), B("M"))
         for j in range(3):
-            tt(nb(j, 1, 2), nb(j, 0, 1), hb("kL", h, j * C, (j + 1) * C), OP.mult)
-        s2 = B(smb(h), 480, 480 + 2 * C)
+            tt(nb(j, 1, 2), nb(j, 0, 1), B("kL", j * C, (j + 1) * C), OP.mult)
         for j in range(3):
-            mm(s2, B("I"), nb(j, 0, 2), j == 0, j == 2)
-        pu = lambda a: hb("pu", h, a * C, (a + 1) * C)
-        fe = hb("fe", h, 3 * C, 4 * C)
-        tt(pu(0), B(smb(h), 480, 480 + C), fe, OP.mult)
-        tt(pu(1), B(smb(h), 480 + C, 480 + 2 * C), pu(0), OP.subtract)
+            mm(B("pb0", 480, 480 + 2 * C), B("I"), nb(j, 0, 2), j == 0, j == 2)
+        pu = lambda a: B("pu", a * C, (a + 1) * C)
+        fe = B("fe", 3 * C, 4 * C)
+        tt(pu(0), B("pb0", 480, 480 + C), fe, OP.mult)
+        tt(pu(1), B("pb0", 480 + C, 480 + 2 * C), pu(0), OP.subtract)
         tt(pu(2), pu(1), fe, OP.add)
-        gtt(hb("eq", h), pu(2), TK(C), B("KIL"), OP.is_equal)
-        gtt(hb("dd", h), hb("nf", h), TK(C), hb("s", h), OP.subtract)
-        tt(hb("ed", h), hb("eq", h), hb("dd", h), OP.mult)
-        tt(hb("s", h), hb("s", h), hb("ed", h), OP.add)
+        gtt(B("eq"), pu(2), B("TK"), B("KIL"), OP.is_equal)
+        gtt(B("dd"), B("nf"), B("TK"), B("s"), OP.subtract)
+        tt(B("ed"), B("eq"), B("dd"), OP.mult)
+        tt(B("s"), B("s"), B("ed"), OP.add)
         if t < VIS - 1:
-            cp(hb("s16", h), hb("s", h))
+            cp(B("s16"), B("s"))
 
-    def near(t, h):
-        cnt = test(t, h, "M_%d" % h, 0, OP.is_le, AF.Sign, -1.0, half, SN)
-        act(hb("nn", h), cnt, AF.Relu, B("thrn"), -1.0)
-        for b in range(NB):
-            bk = rb(h)
-            mm(B(bk, 0, 384), B("I"), B(Ob(t, h), 384 * b, 384 * b + 384), True, False)
-            for a in range(KB):
-                k = KB * b + a
-                mm(B(bk, a * L, (a + 1) * L), B("R", 128 * k, 128 * k + 128), hb("nn", h), False, a == KB - 1)
+    def near(t):
+        cnt = test(t, "M", 0, OP.is_le, AF.Sign, -1.0, half)
+        act(B("nn"), cnt, AF.Relu, B("thrn"), -1.0)
+        for b in range(0, NB, 2):
+            bk = pair()
+            for x in range(2):
+                at = 128 + 384 * x
+                mm(B(bk, at, at + 384), B("I"), B(Ob(t), 384 * (b + x), 384 * (b + x) + 384), True, False)
+                for a in range(2):
+                    k = 2 * (b + x) + a
+                    mm(B(bk, at + a * L, at + (a + 1) * L), B("R", 128 * k, 128 * k + 128), B("nn"), False, a == 1)
             if b == 0:
-                act(hb("acc", h), B(bk, 0, 384), AF.Relu)
+                act(B("acc"), B(bk, 128, 896), AF.Relu)
             else:
-                tt(hb("acc", h), B(bk, 0, 384), hb("acc", h), OP.max)
-        if KB == 4:
-            tt(hb("fo", h), hb("acc", h, 0, 192), hb("acc", h, 192, 384), OP.max)
-            tt(hb("cc", h), hb("fo", h, 0, L), hb("fo", h, L, 2 * L), OP.max)
-        else:
-            tt(hb("cc", h), hb("acc", h, 0, L), hb("acc", h, L, 2 * L), OP.max)
-        tt(hb("cc", h), hb("cc", h), hb("M", h), OP.max)
-        uc = B(umb(h), 496, 496 + C)
-        rows(uc, "SW0", "cc_%d" % h, 0, L)
-        ci = lambda a: hb("ci", h, a * C, (a + 1) * C)
+                tt(B("acc"), B(bk, 128, 896), B("acc"), OP.max)
+        tt(B("fo"), B("acc", 0, 384), B("acc", 384, 768), OP.max)
+        tt(B("cc"), B("fo", 0, L), B("fo", L, 2 * L), OP.max)
+        tt(B("cc"), B("cc"), B("M"), OP.max)
+        uc = B("pbA", 1008, 1008 + C)
+        rows(uc, "SW0", "cc", 0, L)
+        ci = lambda a: B("ci", a * C, (a + 1) * C)
         cp(ci(0), uc)
         tsc(ci(1), ci(0), V - 1, None, OP.bitwise_and)
         tt(ci(2), ci(1), ci(1), OP.mult)
@@ -567,50 +547,43 @@ def build(g, rank, T, topo, report=None):
         tsc(ci(4), ci(2), 5, None, OP.arith_shift_right)
         tt(ci(5), ci(3), ci(4), OP.add)
         tsc(ci(0), ci(5), V - 1, None, OP.bitwise_and)
-        cp(hb("ch", h), ci(0))
-        gtt(hb("df", h), B("CL"), hb("ch", h), hb("cc", h), OP.subtract)
-        act(B(Cb(t + 1, h), 3 * L, 4 * L), hb("df", h), AF.Abs)
+        cp(B("ch"), ci(0))
+        gtt(B("df"), B("CL"), B("ch"), B("cc"), OP.subtract)
+        act(B(Cb(t + 1), 3 * L, 4 * L), B("df"), AF.Abs)
 
-    def visit_bits(t):
-        send("bit", B("bl%d" % (t + 1)), B("bs%d" % (t + 1)), (rank - 1) % N, "ab%d" % (t + 1), 4.0)
-
-    for h in range(H):
-        gather(0, h)
+    gather(0)
+    judge(1)
     for t in range(VIS):
-        for h in range(H):
-            opened(t, h)
-            hashes(t, h)
-            clauses(t, h)
-            trials(t, h)
+        opened(t)
+        cands(t, 0)
+        cands(t, 1)
+        empties(t)
+        for u in range(2):
+            clauses(t, u)
+            trials(t, u)
         if t < VIS - 1:
             visit_bits(t)
         early[0] = LEAD
-        for h in range(H):
-            post(t, h)
+        post(t)
         early[0] = 0.0
-        for h in range(H):
-            near(t, h)
+        near(t)
         if t < VIS - 1:
-            for h in range(H):
-                gather(t + 1, h)
-    dma("Y", ("yx", 0, W, T.yx[:], W), B("X", 0, W), "dyx", 5.0)
+            gather(t + 1)
+
+    dma("Y", D("yx", 0, W), B("X", 0, W), "dyx", 5.0)
     for c2 in range(2):
-        for h in range(H):
-            n = 96 // H
-            cp(B("T3", c2 * 96 + h * n, c2 * 96 + (h + 1) * n), hb("s", h, c2, 16 * C, 2))
+        cp(B("T3", c2 * 96, c2 * 96 + 96), B("s", c2, L, 2))
     for g2 in range(2):
         for c2 in range(2):
-            mm(B("pb3", g2 * 96, g2 * 96 + 96), B("PM%d%d" % (c2, g2)), B("T3", c2 * 96, c2 * 96 + 96), c2 == 0, c2 == 1, True)
+            mm(B("pbR0", g2 * 96, g2 * 96 + 96), B("PM%d%d" % (c2, g2)), B("T3", c2 * 96, c2 * 96 + 96), c2 == 0, c2 == 1, True)
     for g2 in range(2):
         for b in range(6):
-            hh, b1 = b // BH, b % BH
-            cp(B("T4", 32 * b + 16 * g2, 32 * b + 16 * g2 + 16), B("pb3", g2 * 96 + hh * (96 // H) + b1, g2 * 96 + (hh + 1) * (96 // H), BH))
+            cp(B("T4", 32 * b + 16 * g2, 32 * b + 16 * g2 + 16), B("pbR0", g2 * 96 + b, g2 * 96 + 96, 6))
     add("V", lambda: g.vector.transpose(B("T5")[3], B("T4")[3]), [B("T5")], [B("T4")], cyc(192))
     tsc(B("T6"), B("T5"), float(ZB), B("kempty"), OP.is_ge, OP.mult)
     tt(B("T1"), B("T5"), B("T6"), OP.subtract)
-    dma("Y", ("yl", 0, LA, T.yl[:], LA), B("T1"), "dyl", 2.2)
-    for h in range(H):
-        dma("Y", ("yz", h * L, (h + 1) * L, T.yz[:, h * L:(h + 1) * L], L), B(Cb(VIS, h), 3 * L, 4 * L), "dyz%d" % h, 2.2)
+    dma("Y", D("yl", 0, LA), B("T1"), "dyl", 2.2)
+    dma("Y", D("yz", 0, LA), B(Cb(VIS), 3 * L, 4 * L), "dyz", 2.2)
 
     order = schedule(ops)
     emit(g, T, ops, order, sent[0])
@@ -620,37 +593,30 @@ def build(g, rank, T, topo, report=None):
 
 def schedule(ops):
     n = len(ops)
-    succ = [[] for _ in range(n)]
-    left = [0] * n
+    succ, left, tail = [[] for _ in range(n)], [0] * n, [0.0] * n
     for i, o in enumerate(ops):
         left[i] = len(o["deps"])
         for j in o["deps"]:
             succ[j].append(i)
-    tail = [0.0] * n
     for i in range(n - 1, -1, -1):
-        o = ops[i]
-        tail[i] = o["cost"] + o["lat"] + max([tail[s] for s in succ[i]] + [0.0])
+        tail[i] = ops[i]["cost"] + ops[i]["lat"] + max([tail[s] for s in succ[i]] + [0.0])
     for i in range(n):
         tail[i] += ops[i]["early"]
-    free, fin, est = {}, [0.0] * n, [0.0] * n
-    ready = [i for i in range(n) if left[i] == 0]
-    order = []
+    free, est = {}, [0.0] * n
+    ready, order = [i for i in range(n) if left[i] == 0], []
     while ready:
         st = [(max(free.get(ops[i]["eng"], 0.0), est[i]), i) for i in ready]
         t0 = min(st)[0]
-        best = max((tail[i], -i) for s, i in st if s <= t0 + TOL)
-        i = -best[1]
+        i = -max((tail[i], -i) for s, i in st if s <= t0 + TOL)[1]
         o = ops[i]
         s = max(free.get(o["eng"], 0.0), est[i])
-        o["start"] = s
-        free[o["eng"]] = s + o["cost"]
-        fin[i] = s + o["cost"] + o["lat"]
-        o["end"] = s + o["cost"]
+        o["start"], o["end"] = s, s + o["cost"]
+        free[o["eng"]] = o["end"]
         order.append(i)
         ready.remove(i)
         for k in succ[i]:
-            e = fin[i] if (ops[k]["eng"] != o["eng"] or ops[k]["deps"][i]) else o["end"]
-            est[k] = max(est[k], e)
+            wait = ops[k]["eng"] != o["eng"] or ops[k]["deps"][i]
+            est[k] = max(est[k], o["end"] + (o["lat"] if wait else 0.0))
             left[k] -= 1
             if left[k] == 0:
                 ready.append(k)

from concourse.mybir import AluOpType as OP, ActivationFunctionType as AF

N, LA, W, V, VIS = 8, 192, 3072, 4096, 4
A = [6, 4, 4, 3]
ZB = 3072
L, C, W3 = 192, 12, 36
NB = 8
SO = 4
M0 = 10
GRP = ((0, 2), (2, 3))
CHUNKS = (((0, 4), (4, 16)), ((0, 16),))
GV = ((0, 2), ())
TOL, LEAD, LAT = 0.02, 5.0, 0.15
CY, GA = 0.00083, 1.5

SCRATCH = {}
for _t, _l in (
        ("bfloat16", (("X", W + 16), ("CL", V), ("ones", 128), ("neg", 2048), ("R", 2048), ("SLh", 144), ("c8L", W3), ("I", 128), ("nI", 128),
                      ("I64", 128), ("I3", 128), ("I2", 128), ("I1", 128), ("spk", 144), ("SLa", 144), ("SL", 144), ("SLL", 144), ("BOa", 128), ("BO", 128),
                      ("Tri", 128), ("Q16", 128), ("GR", 128), ("GRh", 128), ("LI3b", W3), ("LIb", C), ("c3L", C), ("kpd", 16), ("DX", 576), ("DK", 576),
                      ("Oa", 17 * L), ("Ob", 17 * L), ("Ca", 4 * L), ("Cb", 4 * L), ("cmp", 16 * L), ("op", L), ("le", 3 * L), ("G", 48 * L), ("SG", 16 * L),
                      ("ge", 3 * L), ("nb", 6 * C), ("M", L), ("nn", L), ("acc", 768), ("fo", 384), ("cc", L), ("df", L))),
        ("float32", (("cmk0", 128), ("cmk1", 128), ("PM00", 128), ("PM01", 128), ("PM10", 128), ("PM11", 128), ("p15f", 1), ("kempty", 1), ("thrn", 1),
                     ("thrc", 1), ("cols", 1), ("recb", 12), ("LI3f", W3), ("KIL", L), ("sad", LA), ("sae", LA), ("T1", LA), ("T2", LA), ("T3", LA), ("T4", LA),
                     ("T5", LA), ("T6", LA), ("kpf", 1), ("WK0", 24), ("B0", 12), ("kL", W3), ("pen", W3), ("KU", 576), ("cm", W3), ("cd", 2 * C), ("s", L),
                     ("eq", L), ("dd", L), ("ed", L), ("mx", 15 * C), ("fe", 4 * C), ("pu", 3 * C), ("nf", C))),
        ("int32", (("pc", 1), ("p15", 1), ("g16", 12), ("p15t", 12), ("LI", 12), ("e12", 12), ("q12", 12), ("sln", LA), ("wti", 1), ("kpi", 1),
                   ("ui", W3), ("um", W3), ("sq", W3), ("ba", W3), ("Hs", 576), ("Hm", 576), ("bt", 3 * C), ("ci", 8 * C), ("ni", 2 * C))),
        ("uint16", (("TW", 18), ("TK", 12), ("off", W3), ("ho", 576), ("bo", C), ("ch", C), ("s16", L), ("n16", C)))):
    for _n, _c in _l:
        SCRATCH[_n] = ("sbuf", [128, _c], _t)
for _q in range(1, 5):
    SCRATCH["BK%d" % _q] = ("sbuf", [128, V], "bfloat16")
    SCRATCH["WK%d" % _q] = ("sbuf", [128, 24], "float32")
for _q in range(5):
    SCRATCH["SW%d" % _q] = ("sbuf", [128, 144], "bfloat16")
    SCRATCH["KX%d" % _q] = ("sbuf", [128, 576], "float32")
for _t in range(1, VIS):
    SCRATCH["bs%d" % _t] = ("sbuf", [128, 12], "float32")
    SCRATCH["bl%d" % _t] = ("sbuf", [128, 12], "float32")
for _n, _c in (("pb0", 512), ("pbA", 1024), ("pbR0", 1024), ("pbR1", 1024)):
    SCRATCH[_n] = ("psum", [128, _c], "float32")
OWN = ("X", "CL", "sln", "wti", "kpi", "T1", "WK", "BK", "bs", "bl", "Ca", "Cb", "pb", "pbA", "pbR")
LOGICAL, PLACE, _at = dict(SCRATCH), {}, {}
for _n, (_w, _s, _d) in list(SCRATCH.items()):
    if _n.rstrip("0123456789") in OWN or _n in OWN:
        continue
    _p = "pool_" + _d
    _u = 16 if _d in ("float32", "int32") else 32
    PLACE[_n] = (_p, _at.get(_p, 0))
    _at[_p] = (_at.get(_p, 0) + _s[1] + _u - 1) // _u * _u
    del SCRATCH[_n]
for _p in _at:
    SCRATCH[_p] = ("sbuf", [128, _at[_p]], _p[5:])

SEMAPHORES = ["eV", "eS", "eP", "eG", "sent", "dsl", "dx", "dz", "dcl", "dcm", "dwt", "dkp", "dyx", "dyl", "dyz", "aC1", "aD2", "aD3", "aD4"]
SEMAPHORES += ["aB%d" % q for q in range(1, 5)] + ["aW%d" % q for q in range(1, 5)] + ["ab%d" % t for t in range(1, VIS)]


def rank_program(g, core, T, topo):
    rank = T.rank_of(core)
    if rank is None:
        return
    build(g, rank, T, topo)


def build(g, rank, T, topo, report=None):
    ops, wr, rd, bank, early = [], {}, {}, {}, [0.0]

    def B(name, lo=0, hi=None, step=1, p=(0, 128)):
        if hi is None:
            hi = LOGICAL[name][1][1]
        buf, at = PLACE.get(name, (name, 0))
        x = T[buf][p[0]:p[1], at + lo:at + hi] if step == 1 else T[buf][p[0]:p[1], at + lo:at + hi:step]
        return (name, lo, hi, x, (hi - lo + step - 1) // step)

    def add(eng, call, outs, ins, cost, sem=None, amt=1, lat=LAT):
        i, deps = len(ops), {}

        def dep(j, wait):
            if j != i:
                deps[j] = deps.get(j, False) or wait
        for reg, isw in [(r, False) for r in ins] + [(r, True) for r in outs]:
            name, lo, hi = reg[0], reg[1], reg[2]
            psum = name[:2] == "pb"
            for (a, b, j) in wr.get(name, []):
                if a < hi and lo < b:
                    dep(j, not (psum and eng == "P" and ops[j]["eng"] == "P"))
            if isw:
                for (a, b, j) in rd.get(name, []):
                    if a < hi and lo < b:
                        dep(j, True)
            if psum:
                for b in range(lo // 512, (hi - 1) // 512 + 1):
                    e, run, prev = bank.setdefault((name, b), (eng, [], []))
                    if e != eng:
                        e, run, prev = bank[(name, b)] = (eng, [], run)
                    for j in prev:
                        dep(j, True)
                    if eng == "P" and run:
                        dep(run[-1], False)
                    if i not in run:
                        run.append(i)
        for reg in ins:
            rd.setdefault(reg[0], []).append((reg[1], reg[2], i))
        for reg in outs:
            name, lo, hi = reg[0], reg[1], reg[2]
            if reg[4] == hi - lo:
                wr[name] = [x for x in wr.get(name, []) if not (lo <= x[0] and x[1] <= hi)]
                rd[name] = [x for x in rd.get(name, []) if not (lo <= x[0] and x[1] <= hi)]
            wr.setdefault(name, []).append((lo, hi, i))
        ops.append({"eng": eng, "call": call, "deps": deps, "cost": cost, "sem": sem, "amt": amt, "lat": lat, "early": early[0]})
        return i

    def order_after(i, j):
        ops[i]["deps"].setdefault(j, False)

    def two(*rs):
        return all(LOGICAL[r[0]][2] in ("bfloat16", "uint16") for r in rs)

    def cyc(n):
        return 0.02 + max(64, n) * CY

    def cp(o, i):
        return add("V", lambda: g.vector.tensor_copy(o[3], i[3]), [o], [i], cyc(i[4] * (0.5 if two(o, i) else 1)))

    def tt(o, a, b, op):
        n = a[4] if (a[0][:2] == "pb" or b[0][:2] == "pb") else 2 * a[4]
        return add("V", lambda: g.vector.tensor_tensor(o[3], a[3], b[3], op), [o], [a, b], cyc(n))

    def tsc(o, i, s1, s2, op0, op1=None):
        ins = [i] + [s for s in (s1, s2) if isinstance(s, tuple)]
        v1 = s1[3] if isinstance(s1, tuple) else s1
        v2 = s2[3] if isinstance(s2, tuple) else s2
        if op1 is None:
            f = lambda: g.vector.tensor_scalar(o[3], i[3], v1, None, op0)
        else:
            f = lambda: g.vector.tensor_scalar(o[3], i[3], v1, v2, op0, op1)
        return add("V", f, [o], ins, cyc(i[4] * (0.5 if two(o, i) else 1)))

    def gtt(o, w, off, b, op):
        return add("V", lambda: g.vector.tensor_tensor(o[3], w[3].indirect(off[3]), b[3], op), [o], [w, off, b], 0.05 + o[4] * GA * CY)

    def gcp(o, w, off):
        return add("V", lambda: g.vector.tensor_copy(o[3], w[3].indirect(off[3])), [o], [w, off], 0.05 + o[4] * GA * CY)

    def scat(w, off, i):
        return add("V", lambda: g.vector.tensor_copy(w[3].indirect(off[3]), i[3]), [(w[0], w[1], w[2], w[3], -1)], [off, i], 0.05 + i[4] * 3 * CY)

    def mem(o, c):
        return add("V", lambda: g.vector.memset(o[3], c), [o], [], cyc(o[4] * 0.5))

    def act(o, i, f, bias=None, scale=1.0):
        ins = [i] + [s for s in (bias, scale) if isinstance(s, tuple)]
        if bias is None:
            h = lambda: g.scalar.activation(o[3], i[3], f, scale=scale)
        else:
            h = lambda: g.scalar.activation(o[3], i[3], f, bias=bias[3], scale=scale)
        return add("S", h, [o], ins, 0.05 + max(64, i[4]) * CY)

    def gact(o, w, off):
        return add("S", lambda: g.scalar.activation(o[3], w[3].indirect(off[3]), AF.Copy), [o], [w, off], 0.065 + o[4] * GA * CY)

    def mm(o, l, r, start, stop, f32=False):
        return add("P", lambda: g.tensor.matmul(o[3], l[3], r[3], start, stop), [o], [l, r], max(64, r[4]) * 0.00042 * (4 if f32 else 1))

    E = lambda r, nm="SL": B(nm, 15 - r, 143 - r)

    def rows(o, nm, src, lo, width, extra=()):
        for r in range(16):
            mm(o, E(r, nm), B(src, lo + r, lo + width, 16), r == 0, r == 15 and not extra)
        for x, (l, r) in enumerate(extra):
            mm(o, l, r, False, x == len(extra) - 1)

    def dma(q, o, i, sem, us):
        eng = {"Y": g.sync, "S": g.scalar}[q]
        return add(q, lambda: eng.dma_start(o[3], i[3]), [o] if o[0] in LOGICAL else [], [i] if i[0] in LOGICAL else [], 0.06, sem=sem, amt=16, lat=us)

    def D(name, lo, hi):
        return (name, lo, hi, T[name][:, lo:hi] if hi - lo < T[name].shape[1] else T[name][:], hi - lo)

    sent = [0]

    def send(o, i, dst, sem, us):
        src_core, dst_core = T.cores[rank], T.cores[dst]
        m, n = topo.mask(src_core, dst_core), len(topo.engines(src_core, dst_core))
        rid, pid, _se = topo.addr(dst_core)
        j = add("G", lambda: g.remote_dma(out_ap=o[3], in_ap=i[3], remote_sem=T.sem[sem], local_sem=T.sem.sent, pid=pid, routing_id=rid, dma_engine_mask=m),
                [], [i], 0.5, sem="-", amt=0)
        sent[0] += n
        k = add("R" + sem, None, [o], [], 0.0, sem=sem, amt=n, lat=us)
        ops[k]["deps"][j] = False
        return j

    def asel(o, i, pat, cop, fill, base, cmul):
        return add("G", lambda: g.affine_select(o[3], i[3], pat, cop, fill, base, cmul), [o], [i], 0.17 + 2 * o[4] * CY)

    def iota(o, pat, base, cmul, flag=False):
        if flag:
            f = lambda: g.iota(o[3], pat, base, cmul, allow_small_or_imprecise_dtypes=True)
        else:
            f = lambda: g.iota(o[3], pat, base, cmul)
        return add("G", f, [o], [], 0.13 + 2 * o[4] * CY)

    pairs = [0]

    def pair():
        pairs[0] += 1
        return "pbR%d" % (pairs[0] % 2)

    def clause_order():
        order, vs, ss = [], list(range(M0)), list(range(M0, 16))
        while vs or ss:
            if ss and (not vs or (16 - M0 - len(ss)) * M0 <= (M0 - len(vs)) * (16 - M0)):
                order.append(ss.pop(0))
            else:
                order.append(vs.pop(0))
        return order

    dma("Y", B("sln"), D("sl", 0, LA), "dsl", 2.2)
    dma("S", B("CL", 0, V // 2), D("cl", 0, V // 2), "dcl", 4.0)
    dma("S", B("CL", V // 2, V), D("cl", V // 2, V), "dcm", 6.0)
    dma("Y", B("X", 0, W), D("x0", 0, W), "dx", 5.0)
    dma("Y", B("kpi"), D("kp", 0, 1), "dkp", 2.2)
    dma("Y", B("wti"), D("wt", 0, 1), "dwt", 2.2)
    dma("Y", B("Ca", 3 * L, 4 * L), D("z0", 0, LA), "dz", 2.2)

    mem(B("spk", 0, 144), 0.0)
    mem(B("cmk0"), 0.0)
    mem(B("cmk1"), 0.0)
    mem(B("ones"), 1.0)
    mem(B("spk", 15, 144, 16), 1.0)
    for a in range(4):
        mem(B("cmk0", 32 * a, 32 * a + 16), 1.0)
        mem(B("cmk1", 32 * a + 16, 32 * a + 32), 1.0)
    mem(B("neg"), -512.0)
    iota(B("pc"), [[0, 1]], 0, 1)
    for g2 in range(2):
        for c2 in range(2):
            asel(B("PM%d%d" % (g2, c2)), B("cmk%d" % g2), [[-1, 128]], OP.is_equal, 0.0, 16 * (g2 - c2), 1)
    iota(B("g16"), [[16, 12]], 0, 0)
    asel(B("BOa"), B("ones"), [[-16, 8], [0, 16]], OP.is_ge, 0.0, 0, 1)
    asel(B("BO"), B("BOa"), [[16, 8], [0, 16]], OP.is_ge, 0.0, 15, -1)
    low = (0, 16)
    asel(B("Q16", 0, 128, 1, low), B("ones", 0, 128, 1, low), [[0, 8], [-1, 16]], OP.is_equal, 0.0, 0, 1)
    asel(B("I"), B("ones"), [[-1, 128]], OP.is_equal, 0.0, 0, 1)
    asel(B("SLa"), B("spk"), [[-16, 9], [0, 16]], OP.is_ge, 0.0, 0, 1)
    asel(B("SL"), B("SLa"), [[16, 9], [0, 16]], OP.is_ge, 0.0, 15, -1)
    asel(B("Tri"), B("BO"), [[1, 128]], OP.is_ge, 0.0, 0, -1)
    iota(B("KIL"), [[L, 16], [0, C]], 0, 0, True)
    mm(B("pbR1", 512, 640), B("Q16", 0, 128, 1, low), B("Q16", 0, 128, 1, low), True, True)
    cp(B("GR"), B("pbR1", 512, 640))
    tsc(B("p15"), B("pc"), 15, None, OP.bitwise_and)
    cp(B("p15f"), B("p15"))
    tsc(B("kempty"), B("p15f"), -1.0, float(ZB + 16), OP.mult, OP.add)
    cp(B("sad"), B("sln"))
    tsc(B("sae"), B("sad"), 0.0, B("kempty"), OP.is_lt, OP.mult)
    tt(B("T1"), B("sad"), B("sae"), OP.add)
    add("V", lambda: g.vector.transpose(B("T2")[3], B("T1")[3]), [B("T2")], [B("T1")], cyc(192))
    for g2 in range(2):
        for b in range(6):
            cp(B("T3", g2 * 96 + b, g2 * 96 + 96, 6), B("T2", 32 * b + 16 * g2, 32 * b + 16 * g2 + 16))
    for c2 in range(2):
        for g2 in range(2):
            mm(B("pbR0", c2 * 96, c2 * 96 + 96), B("PM%d%d" % (g2, c2)), B("T3", g2 * 96, g2 * 96 + 96), g2 == 0, g2 == 1, True)
    for c2 in range(2):
        cp(B("s", c2, L, 2), B("pbR0", c2 * 96, c2 * 96 + 96))
    cp(B("s16"), B("s"))
    mem(B("X", W, W + 16), 0.0)
    mem(B("Oa", 16 * L, 17 * L), 0.0)
    mem(B("Ob", 16 * L, 17 * L), 0.0)
    cp(B("WK0", 0, 1), B("wti"))
    cp(B("kpf"), B("kpi"))
    tsc(B("kpd"), B("GR", 0, 16), B("kpf"), None, OP.mult)
    mm(B("pbR1", 0, 16), B("BO"), B("kpd"), True, True)
    cp(B("WK0", 1, 17), B("pbR1", 0, 16))
    cp(B("WK0", 17, 18), B("kpi"))
    mem(B("WK0", 18, 24), 0.0)
    send(B("BK1", 0, V // 2), B("CL", 0, V // 2), (rank - 1) % N, "aC1", 9.0)
    send(B("BK1", V // 2, V), B("CL", V // 2, V), (rank - 1) % N, "aB1", 12.0)
    for q in range(1, 5):
        last = send(B("WK%d" % q), B("WK0"), (rank - q) % N, "aW%d" % q, 4.0)
    order_after(asel(B("R"), B("neg"), [[-1, 16], [-16, 8], [0, 16]], OP.is_equal, 0.0, 0, 1), last)

    def book(q):
        x = 97 * (q - 1)
        a = send(B("BK%d" % q, 0, V - x), B("CL", x, V), (rank - q) % N, "aB%d" % q, 14.0)
        return a, send(B("BK%d" % q, V - x, V), B("CL", 0, x), (rank - q) % N, "aD%d" % q, 14.0)

    book(2)
    tsc(B("nI"), B("I"), -1.0, None, OP.mult)
    tsc(B("GRh"), B("GR"), -0.5, None, OP.mult)
    for nm, v in (("I64", -64.0), ("I3", -3.0 * L), ("I2", -2.0 * L), ("I1", -1.0 * L)):
        tsc(B(nm), B("I"), v, None, OP.mult)
    tsc(B("SLL"), B("SL"), L / 2.0, None, OP.mult)
    tsc(B("SLh"), B("SL"), 0.25, None, OP.mult)
    mem(B("c8L"), 8.0 * L)
    mem(B("c8L", C, 3 * C), 0.0)
    mem(B("p15t"), 0)
    tsc(B("LI"), B("p15t"), B("p15f"), None, OP.add)
    tt(B("LI"), B("LI"), B("g16"), OP.add)
    tsc(B("recb"), B("LI"), 16.0, None, OP.mult)
    for nm, w in (("TW", 2 * C), ("TK", C)):
        tsc(B("q12"), B("LI"), 1.0 / w, -0.5 + 0.5 / w, OP.mult, OP.add)
        tsc(B("e12"), B("q12"), float(-w), None, OP.mult)
        tt(B("q12"), B("e12"), B("LI"), OP.add)
        cp(B(nm, 0, 12), B("q12"))
        if nm == "TW":
            cp(B(nm, 12, 18), B("q12", 0, 6))
    for j in range(3):
        cp(B("LI3f", j * C, (j + 1) * C), B("LI"))
        cp(B("LI3b", j * C, (j + 1) * C), B("LI"))
    cp(B("LIb"), B("LI"))
    mem(B("c3L"), 3.0 * L)
    tsc(B("thrn"), B("p15f"), float(16 - 2 * SO) - 0.5, -3.0, OP.is_ge, OP.mult)
    tsc(B("thrn"), B("thrn"), 12.5, None, OP.add)
    tsc(B("thrc"), B("p15f"), M0 - 0.5, 8.0, OP.is_ge, OP.mult)
    tsc(B("thrc"), B("thrc"), -7.5, None, OP.add)
    mem(B("cols"), 0.5)
    mem(B("B0"), 0.0)
    for a, b in GRP:
        w = (b - a) * C
        for x, m in enumerate(clause_order()):
            lo = 16 * a * C + x * w
            act(B("DX", lo, lo + w), B("LI3f", 0, w), AF.Identity, B("GR", m, m + 1), 0.0)
    tsc(B("SW0"), B("SL"), B("WK0", 0, 1), None, OP.mult)
    half = B("cols")
    Ob = lambda t: "Oa" if t % 2 == 0 else "Ob"
    Cb = lambda t: "Ca" if t % 2 == 0 else "Cb"

    def judge(q):
        tsc(B("SW%d" % q), B("SL"), B("WK%d" % q, 0, 1), None, OP.mult)
        tsc(B("DK"), B("DX"), B("WK%d" % q, 17, 18), None, OP.mult)
        bk = pair()
        for at, lo, hi in ((128, 0, 384), (512, 384, 576)):
            mm(B(bk, at, at + hi - lo), B("BO"), B("DK", lo, hi), True, True)
        act(B("KX%d" % q), B(bk, 128, 704), AF.Copy)

    def gather(t):
        last = {}
        for b in range(NB // 2):
            o, off = B(Ob(t), 768 * b, 768 * b + 768), B("s16", 48 * b, 48 * b + 48)
            j = gcp(o, B("X"), off) if b in GV[min(t, 1)] else gact(o, B("X"), off)
            e = ops[j]["eng"]
            if e in last:
                order_after(j, last[e])
            last[e] = j

    def test(t, src, lo, opv, fS, scale, bias):
        for a in range(2):
            mm(B("pb0", a * L, (a + 1) * L), B("I"), B(src, lo, lo + L), True, True)
        vb, sb, ks = list(range(NB - SO)), list(range(NB - SO, NB, 2)), []
        for x, b in enumerate(vb):
            tt(B("cmp", 384 * b, 384 * b + 384), B(Ob(t), 384 * b, 384 * b + 384), B("pb0", 0, 384), opv)
            ks += [2 * b, 2 * b + 1]
            if x % 2 == 1 and x // 2 < len(sb):
                b = sb[x // 2]
                bk = pair()
                for y in range(2):
                    at = 128 + 384 * y
                    mm(B(bk, at, at + 384), B("I"), B(Ob(t), 384 * (b + y), 384 * (b + y) + 384), True, False)
                    for a in range(2):
                        mm(B(bk, at + a * L, at + (a + 1) * L), B("nI"), B(src, lo, lo + L), False, a == 1)
                act(B("cmp", 384 * b, 384 * b + 768), B(bk, 128, 896), fS, bias, scale)
                ks += range(2 * b, 2 * b + 4)
        cnt = B("pbA", 0, L)
        for x, k in enumerate(ks):
            mm(cnt, E(k), B("cmp", k * L, (k + 1) * L), x == 0, x == 15)
        return cnt

    def opened(t):
        cnt = test(t, Cb(t), 3 * L, OP.is_gt, AF.Relu, 1.0, None)
        act(B("op"), cnt, AF.Sign)
        pr, pv = B("pbA", 800, 800 + L), B("pb0", 0, L)
        mm(pr, B("Tri"), B("op"), True, True)
        mm(pv, B("Tri"), B("op"), True, True)
        act(B("le", 0, L), pr, AF.Sign, half, -1.0)
        for j in (1, 2):
            tsc(B("le", j * L, (j + 1) * L), pv, j + 0.5, 2.0, OP.is_le, OP.mult)

    def small(u):
        n = (GRP[u][1] - GRP[u][0]) * C
        return B("pb0", 384, 384 + n) if u == 0 else B("pbA", 704, 704 + n)

    def cands(t, u):
        zc = Cb(t)
        a, b = GRP[u]
        sl = lambda n: B(n, a * C, b * C)
        o = small(u)
        rows(o, "SLL", "le", a * L, (b - a) * L, ((B("I"), sl("LI3b")), (B("I"), sl("c8L"))))
        cp(sl("off"), o)
        for j in range(a, b):
            gtt(B(zc, j * L, (j + 1) * L), B(Ob(t), 0, 17 * L), B("off", j * C, (j + 1) * C), B(zc, 3 * L, 4 * L), OP.min)
        tt(sl("kL"), o, sl("LI3f"), OP.subtract)
        tsc(sl("pen"), sl("kL"), 15.0 * L, A[t] / 2.0 - 4 - 15.0 * L, OP.max, OP.add)
        o = small(u)
        rows(o, "SW%d" % (t + 1), zc, a * L, (b - a) * L)
        cp(sl("ui"), o)
        tsc(sl("um"), sl("ui"), V - 1, None, OP.bitwise_and)
        tt(sl("sq"), sl("um"), sl("um"), OP.mult)
        tsc(sl("ba"), sl("sq"), 5, None, OP.arith_shift_right)

    def empties(t):
        fe = lambda a: B("fe", a * C, (a + 1) * C)
        m = lambda a, b: B("mx", a * C, b * C)
        tt(m(0, 8), B("s", 0, 8 * C), B("s", 8 * C, 16 * C), OP.max)
        tt(m(8, 12), m(0, 4), m(4, 8), OP.max)
        tt(m(12, 14), m(8, 10), m(10, 12), OP.max)
        tt(m(14, 15), m(12, 13), m(13, 14), OP.max)
        tsc(fe(0), m(14, 15), float(ZB), None, OP.is_ge)
        tsc(fe(1), m(14, 15), -1.0 * L, float(L * (ZB + 15 - t)), OP.mult, OP.add)
        tt(fe(2), fe(0), fe(1), OP.mult)
        tsc(fe(3), fe(2), float(L * t), None, OP.add)

    def clauses(t, u):
        q, cand, order = t + 1, Cb(t), clause_order()
        a, b = GRP[u]
        w, n = (b - a) * C, (b - a) * L
        cnt = B("pbA", 512 * u, 512 * u + n)
        last = None
        for c0, c1 in CHUNKS[u]:
            lo, hi = 16 * a * C + c0 * w, 16 * a * C + c1 * w
            r = lambda nm: B(nm, lo, hi)
            tw = B("TW" if b - a == 2 else "TK", 0, (c1 - c0) * w // 16)
            j = gtt(r("KU"), B("um", a * C, b * C), tw, r("KX%d" % q), OP.mult)
            if last is not None:
                order_after(j, last)
            gtt(r("Hs"), B("ba", a * C, b * C), tw, r("KU"), OP.add)
            tsc(r("Hm"), r("Hs"), V - 1, None, OP.bitwise_and)
            last = cp(r("ho"), r("Hm"))
        sg = 0
        for x, m in enumerate(order):
            off = B("ho", 16 * a * C + x * w, 16 * a * C + (x + 1) * w)
            gm = B("G", m * 3 * L + a * L, m * 3 * L + b * L)
            if m < M0:
                gtt(gm, B("BK%d" % q), off, B(cand, a * L, b * L), OP.is_le)
            else:
                s0 = (sg % 8) * 384
                sg += 1
                gact(B("SG", s0, s0 + n), B("BK%d" % q), off)
                pairs[0] += 1
                bk, at = "pbR%d" % (pairs[0] % 2), 512 * (pairs[0] // 2 % 2)
                mm(B(bk, at, at + n), B("I"), B("SG", s0, s0 + n), True, False)
                mm(B(bk, at, at + n), B("nI"), B(cand, a * L, b * L), False, True)
                act(gm, B(bk, at, at + n), AF.Sign, half, -1.0)
            mm(cnt, E(m), gm, x == 0, x == 15)
        act(B("ge", a * L, b * L), cnt, AF.Sign, B("thrc"))
        if u == 0 and t < VIS - 1:
            judge(q + 1)
        rows(small(u), "SLh", "ge", a * L, n)

    def trials(t, u):
        nj = lambda j: B("nb", 2 * j * C, (2 * j + 1) * C)
        a, b = GRP[u]
        cn = small(u)
        x = 0
        if u == 0:
            thr, x = B("cd", 0, C), C
            tt(thr, B("pen", 0, C), B("B0") if t == 0 else B("bl%d" % t), OP.add)
            tt(nj(0), B(cn[0], cn[1], cn[1] + C), thr, OP.is_ge)
        tt(B("cm", a * C + x, b * C), B(cn[0], cn[1] + x, cn[2]), B("pen", a * C + x, b * C), OP.subtract)
        pn, pd = B("pb0", 432, 432 + C), B("pb0", 448, 448 + C)
        for j in range(a, b):
            if j:
                qn, d = B("bt", (j - 1) * C, j * C), B("cd", C, 2 * C)
                tsc(qn, pn, 0.25, None, OP.add)
                tt(d, B("cm", j * C, (j + 1) * C), pd, OP.add)
                tt(nj(j), d, qn, OP.is_ge)
            if j < 2 or t < VIS - 1:
                mm(pn, B("GRh"), nj(j), True, True)
            if j < 2:
                mm(pd, B("GRh"), nj(j), True, False)
                for i in range(j + 1):
                    mm(pd, B("I64"), nj(i), False, i == j)
        if b < 3:
            return
        bo = B("pb0", 464, 464 + C)
        mm(bo, B("I"), B("LIb"), True, False)
        mm(bo, B("I"), B("c3L"), False, False)
        for j in range(3):
            mm(bo, B("I%d" % (3 - j)), nj(j), False, j == 2)
        x = cp(B("bo"), bo)
        if t < VIS - 1:
            pi, pj = B("bt", 2 * C, 3 * C), B("ci", 6 * C, 7 * C)
            order_after(tsc(pi, pn, -2.0, None, OP.mult), x)
            tsc(pj, pi, 1, None, OP.bitwise_and)
            tsc(B("bs%d" % (t + 1)), pj, 0.5, None, OP.mult)
        gact(B("M"), B(Cb(t), 0, 4 * L), B("bo"))

    def visit_bits(t):
        k = send(B("bl%d" % (t + 1)), B("bs%d" % (t + 1)), (rank - 1) % N, "ab%d" % (t + 1), 4.0)
        if t < 2:
            for b in book(t + 3):
                order_after(b, k)

    def post(t):
        nb = lambda j, a, b: B("nb", (2 * j + a) * C, (2 * j + b) * C)
        um = B("pbA", 992, 992 + C)
        rows(um, "SW0", "M", 0, L)
        ni = lambda a: B("ni", a * C, (a + 1) * C)
        cp(ni(0), um)
        tsc(ni(1), ni(0), 15, None, OP.bitwise_and)
        tt(B("nf"), ni(1), B("recb"), OP.add)
        cp(B("n16"), B("nf"))
        scat(B("X"), B("n16"), B("M"))
        for j in range(3):
            tt(nb(j, 1, 2), nb(j, 0, 1), B("kL", j * C, (j + 1) * C), OP.mult)
        for j in range(3):
            mm(B("pb0", 480, 480 + 2 * C), B("I"), nb(j, 0, 2), j == 0, j == 2)
        pu = lambda a: B("pu", a * C, (a + 1) * C)
        fe = B("fe", 3 * C, 4 * C)
        tt(pu(0), B("pb0", 480, 480 + C), fe, OP.mult)
        tt(pu(1), B("pb0", 480 + C, 480 + 2 * C), pu(0), OP.subtract)
        tt(pu(2), pu(1), fe, OP.add)
        gtt(B("eq"), pu(2), B("TK"), B("KIL"), OP.is_equal)
        gtt(B("dd"), B("nf"), B("TK"), B("s"), OP.subtract)
        tt(B("ed"), B("eq"), B("dd"), OP.mult)
        tt(B("s"), B("s"), B("ed"), OP.add)
        if t < VIS - 1:
            cp(B("s16"), B("s"))

    def near(t):
        cnt = test(t, "M", 0, OP.is_le, AF.Sign, -1.0, half)
        act(B("nn"), cnt, AF.Relu, B("thrn"), -1.0)
        for b in range(0, NB, 2):
            bk = pair()
            for x in range(2):
                at = 128 + 384 * x
                mm(B(bk, at, at + 384), B("I"), B(Ob(t), 384 * (b + x), 384 * (b + x) + 384), True, False)
                for a in range(2):
                    k = 2 * (b + x) + a
                    mm(B(bk, at + a * L, at + (a + 1) * L), B("R", 128 * k, 128 * k + 128), B("nn"), False, a == 1)
            if b == 0:
                act(B("acc"), B(bk, 128, 896), AF.Relu)
            else:
                tt(B("acc"), B(bk, 128, 896), B("acc"), OP.max)
        tt(B("fo"), B("acc", 0, 384), B("acc", 384, 768), OP.max)
        tt(B("cc"), B("fo", 0, L), B("fo", L, 2 * L), OP.max)
        tt(B("cc"), B("cc"), B("M"), OP.max)
        uc = B("pbA", 1008, 1008 + C)
        rows(uc, "SW0", "cc", 0, L)
        ci = lambda a: B("ci", a * C, (a + 1) * C)
        cp(ci(0), uc)
        tsc(ci(1), ci(0), V - 1, None, OP.bitwise_and)
        tt(ci(2), ci(1), ci(1), OP.mult)
        tsc(ci(3), ci(1), B("WK0", 1, 2), 97.0 * t, OP.mult, OP.add)
        tsc(ci(4), ci(2), 5, None, OP.arith_shift_right)
        tt(ci(5), ci(3), ci(4), OP.add)
        tsc(ci(0), ci(5), V - 1, None, OP.bitwise_and)
        cp(B("ch"), ci(0))
        gtt(B("df"), B("CL"), B("ch"), B("cc"), OP.subtract)
        act(B(Cb(t + 1), 3 * L, 4 * L), B("df"), AF.Abs)

    gather(0)
    judge(1)
    for t in range(VIS):
        opened(t)
        cands(t, 0)
        cands(t, 1)
        empties(t)
        for u in range(2):
            clauses(t, u)
            trials(t, u)
        if t < VIS - 1:
            visit_bits(t)
        early[0] = LEAD
        post(t)
        early[0] = 0.0
        near(t)
        if t < VIS - 1:
            gather(t + 1)

    dma("Y", D("yx", 0, W), B("X", 0, W), "dyx", 5.0)
    for c2 in range(2):
        cp(B("T3", c2 * 96, c2 * 96 + 96), B("s", c2, L, 2))
    for g2 in range(2):
        for c2 in range(2):
            mm(B("pbR0", g2 * 96, g2 * 96 + 96), B("PM%d%d" % (c2, g2)), B("T3", c2 * 96, c2 * 96 + 96), c2 == 0, c2 == 1, True)
    for g2 in range(2):
        for b in range(6):
            cp(B("T4", 32 * b + 16 * g2, 32 * b + 16 * g2 + 16), B("pbR0", g2 * 96 + b, g2 * 96 + 96, 6))
    add("V", lambda: g.vector.transpose(B("T5")[3], B("T4")[3]), [B("T5")], [B("T4")], cyc(192))
    tsc(B("T6"), B("T5"), float(ZB), B("kempty"), OP.is_ge, OP.mult)
    tt(B("T1"), B("T5"), B("T6"), OP.subtract)
    dma("Y", D("yl", 0, LA), B("T1"), "dyl", 2.2)
    dma("Y", D("yz", 0, LA), B(Cb(VIS), 3 * L, 4 * L), "dyz", 2.2)

    order = schedule(ops)
    emit(g, T, ops, order, sent[0])
    if report is not None:
        report.append((ops, order))


def schedule(ops):
    n = len(ops)
    succ, left, tail = [[] for _ in range(n)], [0] * n, [0.0] * n
    for i, o in enumerate(ops):
        left[i] = len(o["deps"])
        for j in o["deps"]:
            succ[j].append(i)
    for i in range(n - 1, -1, -1):
        tail[i] = ops[i]["cost"] + ops[i]["lat"] + max([tail[s] for s in succ[i]] + [0.0])
    for i in range(n):
        tail[i] += ops[i]["early"]
    free, est = {}, [0.0] * n
    ready, order = [i for i in range(n) if left[i] == 0], []
    while ready:
        st = [(max(free.get(ops[i]["eng"], 0.0), est[i]), i) for i in ready]
        t0 = min(st)[0]
        i = -max((tail[i], -i) for s, i in st if s <= t0 + TOL)[1]
        o = ops[i]
        s = max(free.get(o["eng"], 0.0), est[i])
        o["start"], o["end"] = s, s + o["cost"]
        free[o["eng"]] = o["end"]
        order.append(i)
        ready.remove(i)
        for k in succ[i]:
            wait = ops[k]["eng"] != o["eng"] or ops[k]["deps"][i]
            est[k] = max(est[k], o["end"] + (o["lat"] if wait else 0.0))
            left[k] -= 1
            if left[k] == 0:
                ready.append(k)
    return order


def emit(g, T, ops, order, nsent):
    queue = {"V": g.vector, "S": g.scalar, "P": g.tensor, "G": g, "Y": g.sync}
    need = set()
    for o in ops:
        for j, w in o["deps"].items():
            if w:
                need.add(j)
    total, mark, know, snap = {}, {}, {}, {}
    for i in order:
        o = ops[i]
        e = o["eng"]
        if e[0] == "R":
            total[o["sem"]] = o["amt"]
            mark[i] = (o["sem"], o["amt"])
            snap[i] = {}
            continue
        k = know.setdefault(e, {})
        want = {}
        for j, w in o["deps"].items():
            if w:
                s, v = mark[j]
                if k.get(s, 0) < v and want.get(s, (0, 0))[0] < v:
                    want[s] = (v, j)
        for s in list(want):
            if any(s2 != s and snap[want[s2][1]].get(s, 0) >= want[s][0] for s2 in want):
                del want[s]
        for s, (v, j) in want.items():
            queue[e].wait_ge(T.sem[s], v)
            k[s] = max(k.get(s, 0), v)
            for s2, v2 in snap[j].items():
                k[s2] = max(k.get(s2, 0), v2)
        ins = o["call"]()
        if o["sem"] == "-":
            continue
        if o["sem"] is not None:
            ins.then_inc(T.sem[o["sem"]], o["amt"])
            total[o["sem"]] = o["amt"]
            mark[i] = (o["sem"], o["amt"])
        elif i in need:
            s = "e" + e
            ins.then_inc(T.sem[s], 1)
            total[s] = total.get(s, 0) + 1
            mark[i] = (s, total[s])
        else:
            continue
        snap[i] = dict(k)
    for s, v in total.items():
        if know.get("G", {}).get(s, 0) < v:
            g.wait_ge(T.sem[s], v)
    g.wait_ge(T.sem.sent, nsent)
